import numpy as np
import ml_dtypes


def mxq(x, axis, fmt="e4m3"):
    dtype, down = {"e4m3": (ml_dtypes.float8_e4m3fn, 7), "e5m2": (ml_dtypes.float8_e5m2, 14)}[fmt]
    v = np.moveaxis(np.asarray(x, np.float32).astype(ml_dtypes.bfloat16).astype(np.float64), axis, -1)
    blocks = v.reshape(v.shape[:-1] + (-1, 32))
    amax = np.abs(blocks).max(-1, keepdims=True)
    byte = np.maximum(np.where(amax > 0, np.frexp(amax)[1] - 1 + 127, 0) - down, 1)
    scale = np.exp2(byte - 127.0)
    codes = (blocks / scale).astype(np.float32).astype(dtype).astype(np.float64)
    return np.moveaxis((codes * scale).reshape(v.shape), -1, axis)


WIDE = False


def mx_kscale(k):
    if not WIDE:
        return np.ones(k)
    levels = np.array([18, -18])
    if k % 512:
        return np.exp2(np.random.permutation(np.resize(levels, k // 32))).repeat(32)
    a = np.empty((k // 512, 16))
    for p in range(k // 512):
        a[p, :8] = np.random.permutation(np.resize(levels, 8))
        for g in range(8):
            far = levels[np.abs(levels - a[p, g]) >= 10]
            a[p, g + 8] = far[np.random.randint(len(far))]
    return np.exp2(a.ravel()).repeat(32)


def f64(x):
    return np.asarray(x).astype(np.float64)


def striped(idx):
    return np.tile(np.asarray(idx).reshape(-1, 16).T, (8, 1)).astype(np.uint16)


def unstriped(offs):
    return offs[:16].T.reshape(-1).astype(np.int64)


B, N, T, D, DV, NQ = 1, 512, 1024, 128, 0, 1024


def setup_inputs():
    n = np.random.standard_normal
    idx = np.sort(np.random.permutation(T)[:B * N].reshape(B, N), axis=1).reshape(-1)
    z = mx_kscale(NQ)[:, None]
    return {
        "g": (n((B, NQ, N)) * z / np.sqrt(NQ)).astype(np.float32),
        "qm": (n((B, NQ, D)) / z).astype(np.float32),
        "offs": striped(idx),
    }


def reference(g, qm, offs):
    idx = unstriped(offs)
    dk = mxq(f64(qm), 1, "e4m3").transpose(0, 2, 1) @ mxq(f64(g), 1, "e5m2")
    out = np.zeros((D, T))
    out[:, idx] = dk.transpose(1, 0, 2).reshape(D, B * N)
    return out

@@ -1,0 +1,110 @@
+from contextlib import ExitStack
+
+import concourse.mybir as mybir
+
+Q, SLOTS, TOKENS, D = 1024, 512, 1024, 128
+
+FLOPS = 2 * Q * SLOTS * D
+
+F32 = mybir.dt.float32
+BF16 = mybir.dt.bfloat16
+U32 = mybir.dt.uint32
+U16 = mybir.dt.uint16
+U8 = mybir.dt.uint8
+E4M3X4 = mybir.dt.float8_e4m3fn_x4
+E5M2X4 = mybir.dt.float8_e5m2_x4
+
+P = 128
+PACK = 4
+PASSES = Q // (P * PACK)
+
+
+def tile_attend_dk_kernel(tc, g, qm, offs, out):
+    nc = tc.nc
+    g_rows = g.rearrange("b (c p j) n -> (b c) p j n", p=P, j=PACK)
+    qm_rows = qm.rearrange("b (c p j) d -> (b c) p j d", p=P, j=PACK)
+
+    with ExitStack() as ctx:
+        held = ctx.enter_context(tc.tile_pool(name="held", bufs=1))
+        psum = ctx.enter_context(tc.psum_pool(name="psum", bufs=1))
+
+        offsets = held.tile([P, SLOTS // 16], U16, name="offsets")
+        placed = held.tile([P, TOKENS], F32, name="placed")
+        sums = held.tile([P, SLOTS], F32, name="sums")
+        acc = psum.tile([D, SLOTS], F32, name="acc")
+
+        def load(rows, width, name):
+            raw = held.tile([P, PACK, width], F32, name=name)
+            nc.sync.dma_start(out=raw[:], in_=rows)
+            return raw
+
+        def load_pair(c, h):
+            raw = held.tile([P, 2, SLOTS], F32, name=f"g_raw{c}{h}")
+            nc.sync.dma_start(out=raw[:], in_=g_rows[c][:, 2 * h : 2 * h + 2, :])
+            return raw
+
+        q_raw0 = load(qm_rows[0], D, "q_raw0")
+        g_raw = [[load_pair(c, h) for h in range(2)] for c in range(PASSES)]
+        q_raw1 = load(qm_rows[1], D, "q_raw1")
+        nc.sync.dma_start(offsets[:], offs)
+
+        nc.vector.memset(placed[:], 0.0)
+
+        g_codes = [held.tile([P, SLOTS], U32, name=f"g_codes{c}", align_bytes=64) for c in range(PASSES)]
+        g_scales = [held.tile([P, SLOTS], U8, name=f"g_scales{c}", align_bytes=64) for c in range(PASSES)]
+        q_codes = [held.tile([P, D], U32, name=f"q_codes{c}", align_bytes=64) for c in range(PASSES)]
+        q_scales = [held.tile([P, D], U8, name=f"q_scales{c}", align_bytes=64) for c in range(PASSES)]
+
+        def quantize(grouped, codes, scales, lo, hi, dtype):
+            nc.vector.quantize_mx(
+                out=codes[:, lo:hi].bitcast(dtype),
+                scales=scales[:, lo:hi],
+                in_=grouped[:, lo:hi, :].rearrange("p w j -> p (w j)"),
+            )
+
+        def multiply(c):
+            nc.tensor.matmul_mx(
+                out=acc[:],
+                lhsT=q_codes[c][:].bitcast(E4M3X4),
+                lhsT_scale=q_scales[c][:],
+                rhs=g_codes[c][:].bitcast(E5M2X4),
+                rhs_scale=g_scales[c][:],
+                start=(c == 0),
+                stop=(c == PASSES - 1),
+            )
+
+        v, s = nc.vector.tensor_copy, nc.scalar.copy
+        HALF = SLOTS // 2
+        gb = [held.tile([P, SLOTS, PACK], BF16, name=f"gb{c}", align_bytes=64) for c in range(PASSES)]
+        qb = [held.tile([P, D, PACK], BF16, name=f"qb{c}", align_bytes=64) for c in range(PASSES)]
+
+        def cast_pair(c, h, cut):
+            planes = slice(2 * h, 2 * h + 2)
+            v(gb[c][:, :cut, planes], g_raw[c][h][:, :, :cut].rearrange("p j w -> p w j"))
+            s(gb[c][:, cut:, planes], g_raw[c][h][:, :, cut:].rearrange("p j w -> p w j"))
+
+        def cast_q(c, raw, copy):
+            copy(
+                qb[c][:].rearrange("p (b i) j -> p b j i", i=4),
+                raw[:].rearrange("p j (b i) -> p b j i", i=4),
+            )
+
+        cast_q(0, q_raw0, v)
+        quantize(qb[0], q_codes[0], q_scales[0], 0, D, E4M3X4)
+        cast_pair(0, 0, HALF)
+        cast_pair(0, 1, HALF)
+        quantize(gb[0], g_codes[0], g_scales[0], 0, HALF, E5M2X4)
+        quantize(gb[0], g_codes[0], g_scales[0], HALF, SLOTS, E5M2X4)
+        multiply(0)
+        cast_pair(1, 0, HALF)
+        cast_pair(1, 1, 320)
+        cast_q(1, q_raw1, s)
+        quantize(gb[1], g_codes[1], g_scales[1], 0, HALF, E5M2X4)
+        quantize(qb[1], q_codes[1], q_scales[1], 0, D, E4M3X4)
+        quantize(gb[1], g_codes[1], g_scales[1], HALF, SLOTS, E5M2X4)
+        multiply(1)
+
+        for lo, hi in ((0, 512),):
+            nc.scalar.copy(sums[:, lo:hi], acc[:, lo:hi])
+            nc.vector.tensor_copy(placed[:].indirect(offsets[:, lo // 16 : hi // 16]), sums[:, lo:hi])
+        nc.sync.dma_start(out=out, in_=placed[:])

@@ -1,6 +1,7 @@
 from contextlib import ExitStack
 
 import concourse.mybir as mybir
+from concourse.masks import make_identity
 
 Q, SLOTS, TOKENS, D = 1024, 512, 1024, 128
 
@@ -89,13 +90,25 @@ def tile_attend_dk_kernel(tc, g, qm, offs, out):
                 raw[:].rearrange("p j (b i) -> p b j i", i=4),
             )
 
+        identity = held.tile([P, P], F32, name="identity")
+        make_identity(nc, identity[:])
+        spare = [psum.tile([P, 4, P], F32, name=f"spare{b}") for b in range(6)]
+
+        def warm(raw, bank):
+            for t in range(4):
+                nc.tensor.transpose(spare[bank][:, t, :], raw[:, bank % 2, t * P : (t + 1) * P], identity[:])
+
         cast_q(0, q_raw0, v)
+        for bank in range(4):
+            warm(g_raw[0][bank // 2], bank)
         quantize(qb[0], q_codes[0], q_scales[0], 0, D, E4M3X4)
         cast_pair(0, 0, HALF)
         cast_pair(0, 1, HALF)
         quantize(gb[0], g_codes[0], g_scales[0], 0, HALF, E5M2X4)
         quantize(gb[0], g_codes[0], g_scales[0], HALF, SLOTS, E5M2X4)
+        warm(g_raw[1][0], 4)
         multiply(0)
+        warm(g_raw[1][1], 5)
         cast_pair(1, 0, HALF)
         cast_pair(1, 1, 320)
         cast_q(1, q_raw1, s)

@@ -92,23 +92,25 @@ def tile_attend_dk_kernel(tc, g, qm, offs, out):
 
         identity = held.tile([P, P], F32, name="identity")
         make_identity(nc, identity[:])
-        spare = [psum.tile([P, 4, P], F32, name=f"spare{b}") for b in range(6)]
+        spare = [psum.tile([P, SLOTS], F32, name=f"spare{b}") for b in range(7)]
 
-        def warm(raw, bank):
-            for t in range(4):
-                nc.tensor.transpose(spare[bank][:, t, :], raw[:, bank % 2, t * P : (t + 1) * P], identity[:])
+        def warm(raw, banks):
+            for j, bank in enumerate(banks):
+                for t in range(4):
+                    cols = slice(t * P, (t + 1) * P)
+                    nc.tensor.transpose(bank[:, cols], raw[:, j, cols], identity[:])
 
+        warm(g_raw[0][0], spare[0:2])
+        warm(g_raw[0][1], spare[2:4])
+        warm(g_raw[1][0], [spare[4], acc])
         cast_q(0, q_raw0, v)
-        for bank in range(4):
-            warm(g_raw[0][bank // 2], bank)
         quantize(qb[0], q_codes[0], q_scales[0], 0, D, E4M3X4)
         cast_pair(0, 0, HALF)
         cast_pair(0, 1, HALF)
         quantize(gb[0], g_codes[0], g_scales[0], 0, HALF, E5M2X4)
         quantize(gb[0], g_codes[0], g_scales[0], HALF, SLOTS, E5M2X4)
-        warm(g_raw[1][0], 4)
         multiply(0)
-        warm(g_raw[1][1], 5)
+        warm(g_raw[1][1], spare[5:7])
         cast_pair(1, 0, HALF)
         cast_pair(1, 1, 320)
         cast_q(1, q_raw1, s)

@@ -34,27 +34,18 @@ def tile_attend_dk_kernel(tc, g, qm, offs, out):
         sums = held.tile([P, SLOTS], F32, name="sums")
         acc = psum.tile([D, SLOTS], F32, name="acc")
 
-        def load(rows, width, name):
-            raw = held.tile([P, PACK, width], F32, name=name)
+        def load(rows, name):
+            raw = held.tile([P, rows.shape[1], rows.shape[2]], F32, name=name)
             nc.sync.dma_start(out=raw[:], in_=rows)
             return raw
-
-        def load_pair(c, h):
-            raw = held.tile([P, 2, SLOTS], F32, name=f"g_raw{c}{h}")
-            nc.sync.dma_start(out=raw[:], in_=g_rows[c][:, 2 * h : 2 * h + 2, :])
-            return raw
-
-        q_raw0 = load(qm_rows[0], D, "q_raw0")
-        g_raw = [[load_pair(c, h) for h in range(2)] for c in range(PASSES)]
-        q_raw1 = load(qm_rows[1], D, "q_raw1")
-        nc.sync.dma_start(offsets[:], offs)
-
-        nc.vector.memset(placed[:], 0.0)
 
         g_codes = [held.tile([P, SLOTS], U32, name=f"g_codes{c}", align_bytes=64) for c in range(PASSES)]
         g_scales = [held.tile([P, SLOTS], U8, name=f"g_scales{c}", align_bytes=64) for c in range(PASSES)]
         q_codes = [held.tile([P, D], U32, name=f"q_codes{c}", align_bytes=64) for c in range(PASSES)]
         q_scales = [held.tile([P, D], U8, name=f"q_scales{c}", align_bytes=64) for c in range(PASSES)]
+        gb = [held.tile([P, SLOTS, PACK], BF16, name=f"gb{c}", align_bytes=64) for c in range(PASSES)]
+        qb = [held.tile([P, D, PACK], BF16, name=f"qb{c}", align_bytes=64) for c in range(PASSES)]
+        v, s = nc.vector.tensor_copy, nc.scalar.copy
 
         def quantize(grouped, codes, scales, lo, hi, dtype):
             nc.vector.quantize_mx(
@@ -62,6 +53,12 @@ def tile_attend_dk_kernel(tc, g, qm, offs, out):
                 scales=scales[:, lo:hi],
                 in_=grouped[:, lo:hi, :].rearrange("p w j -> p (w j)"),
             )
+
+        def quantize_g(c, lo, hi):
+            quantize(gb[c], g_codes[c], g_scales[c], lo, hi, E5M2X4)
+
+        def quantize_q(c):
+            quantize(qb[c], q_codes[c], q_scales[c], 0, D, E4M3X4)
 
         def multiply(c):
             nc.tensor.matmul_mx(
@@ -74,21 +71,23 @@ def tile_attend_dk_kernel(tc, g, qm, offs, out):
                 stop=(c == PASSES - 1),
             )
 
-        v, s = nc.vector.tensor_copy, nc.scalar.copy
-        HALF = SLOTS // 2
-        gb = [held.tile([P, SLOTS, PACK], BF16, name=f"gb{c}", align_bytes=64) for c in range(PASSES)]
-        qb = [held.tile([P, D, PACK], BF16, name=f"qb{c}", align_bytes=64) for c in range(PASSES)]
-
-        def cast_pair(c, h, cut):
-            planes = slice(2 * h, 2 * h + 2)
-            v(gb[c][:, :cut, planes], g_raw[c][h][:, :, :cut].rearrange("p j w -> p w j"))
-            s(gb[c][:, cut:, planes], g_raw[c][h][:, :, cut:].rearrange("p j w -> p w j"))
-
-        def cast_q(c, raw, copy):
+        def cast_words(copy, grouped, raw, first, lo, hi):
             copy(
-                qb[c][:].rearrange("p (b i) j -> p b j i", i=4),
-                raw[:].rearrange("p j (b i) -> p b j i", i=4),
+                grouped[:, first + lo : first + hi, :].rearrange("p (b i) j -> p b j i", i=4),
+                raw[:, :, lo:hi].rearrange("p j (b i) -> p b j i", i=4),
             )
+
+        def cast_pair(copy, grouped, raw, h, first, lo, hi):
+            copy(
+                grouped[:, first + lo : first + hi, 2 * h : 2 * h + 2],
+                raw[:, :, lo:hi].rearrange("p j w -> p w j"),
+            )
+
+        g_raw = [[load(g_rows[c][:, 2 * h : 2 * h + 2, :], f"g_raw{c}{h}") for h in range(2)] for c in range(PASSES)]
+        q_raw = [load(qm_rows[c], f"q_raw{c}") for c in range(PASSES)]
+        nc.sync.dma_start(offsets[:], offs)
+
+        nc.vector.memset(placed[:], 0.0)
 
         identity = held.tile([P, P], F32, name="identity")
         make_identity(nc, identity[:])
@@ -102,24 +101,31 @@ def tile_attend_dk_kernel(tc, g, qm, offs, out):
 
         warm(g_raw[0][0], spare[0:2])
         warm(g_raw[0][1], spare[2:4])
-        warm(g_raw[1][0], [spare[4], acc])
-        cast_q(0, q_raw0, v)
-        quantize(qb[0], q_codes[0], q_scales[0], 0, D, E4M3X4)
-        cast_pair(0, 0, HALF)
-        cast_pair(0, 1, HALF)
-        quantize(gb[0], g_codes[0], g_scales[0], 0, HALF, E5M2X4)
-        quantize(gb[0], g_codes[0], g_scales[0], HALF, SLOTS, E5M2X4)
+        warm(g_raw[1][0], spare[4:6])
+        warm(g_raw[1][1], [spare[6], acc])
+
+        def cast_g(c, h, cut):
+            cast_pair(v, gb[c], g_raw[c][h], h, 0, 0, cut)
+            cast_pair(s, gb[c], g_raw[c][h], h, 0, cut, SLOTS)
+
+        cast_g(0, 0, 256)
+        cast_g(0, 1, 256)
+        quantize_g(0, 0, 256)
+        quantize_g(0, 256, SLOTS)
+        cast_g(1, 0, 256)
+        cast_pair(v, gb[1], g_raw[1][1], 1, 0, 0, 256)
+        cast_pair(s, gb[1], g_raw[1][1], 1, 0, 384, SLOTS)
+        cast_pair(v, gb[1], g_raw[1][1], 1, 0, 256, 384)
+        quantize_g(1, 0, 256)
+        quantize_g(1, 256, SLOTS)
+        cast_words(s, qb[0], q_raw[0], 0, 0, D)
+        cast_words(v, qb[1], q_raw[1], 0, 0, 48)
+        quantize_q(0)
         multiply(0)
-        warm(g_raw[1][1], spare[5:7])
-        cast_pair(1, 0, HALF)
-        cast_pair(1, 1, 320)
-        cast_q(1, q_raw1, s)
-        quantize(gb[1], g_codes[1], g_scales[1], 0, HALF, E5M2X4)
-        quantize(qb[1], q_codes[1], q_scales[1], 0, D, E4M3X4)
-        quantize(gb[1], g_codes[1], g_scales[1], HALF, SLOTS, E5M2X4)
+        cast_words(s, qb[1], q_raw[1], 0, 48, D)
+        quantize_q(1)
         multiply(1)
 
-        for lo, hi in ((0, 512),):
-            nc.scalar.copy(sums[:, lo:hi], acc[:, lo:hi])
-            nc.vector.tensor_copy(placed[:].indirect(offsets[:, lo // 16 : hi // 16]), sums[:, lo:hi])
+        nc.scalar.copy(sums[:], acc[:])
+        nc.vector.tensor_copy(placed[:].indirect(offsets[:]), sums[:])
         nc.sync.dma_start(out=out, in_=placed[:])

@@ -89,20 +89,27 @@ def tile_attend_dk_kernel(tc, g, qm, offs, out):
 
         nc.vector.memset(placed[:], 0.0)
 
-        identity = held.tile([P, P], F32, name="identity")
-        make_identity(nc, identity[:])
-        spare = [psum.tile([P, SLOTS], F32, name=f"spare{b}") for b in range(7)]
+        identity_bf16 = held.tile([P, P], BF16, name="identity_bf16")
+        identity_f32 = held.tile([P, P], F32, name="identity_f32")
+        make_identity(nc, identity_bf16[:])
+        make_identity(nc, identity_f32[:])
+        spare_bf16 = [psum.tile([P, 4, P], BF16, name=f"spare_bf16{b}") for b in range(4)]
+        spare_f32 = [psum.tile([P, SLOTS], F32, name=f"spare_f32{b}") for b in range(3)]
+
+        for i in range(32):
+            nc.tensor.transpose(spare_bf16[i // 4 % 4][:, i % 4, :], identity_bf16[:], identity_bf16[:])
 
         def warm(raw, banks):
-            for j, bank in enumerate(banks):
-                for t in range(4):
-                    cols = slice(t * P, (t + 1) * P)
-                    nc.tensor.transpose(bank[:, cols], raw[:, j, cols], identity[:])
+            words = raw[:].rearrange("p j w -> p (j w)")
+            blocks = words.shape[1] // P
+            for i in range(4 * len(banks)):
+                first = i % blocks * P
+                nc.tensor.transpose(banks[i // 4][:, i % 4 * P : (i % 4 + 1) * P], words[:, first : first + P], identity_f32[:])
 
-        warm(g_raw[0][0], spare[0:2])
-        warm(g_raw[0][1], spare[2:4])
-        warm(g_raw[1][0], spare[4:6])
-        warm(g_raw[1][1], [spare[6], acc])
+        warm(g_raw[0][1], spare_f32[:3])
+        warm(g_raw[1][0], spare_f32[:3])
+        warm(g_raw[1][1], spare_f32[:3])
+        warm(q_raw[0], [spare_f32[0], acc])
 
         def cast_g(c, h, cut):
             cast_pair(v, gb[c], g_raw[c][h], h, 0, 0, cut)

@@ -120,11 +120,12 @@ def tile_attend_dk_kernel(tc, g, qm, offs, out):
         quantize_g(0, 0, 256)
         quantize_g(0, 256, SLOTS)
         cast_g(1, 0, 256)
-        cast_pair(v, gb[1], g_raw[1][1], 1, 0, 0, 256)
-        cast_pair(s, gb[1], g_raw[1][1], 1, 0, 384, SLOTS)
-        cast_pair(v, gb[1], g_raw[1][1], 1, 0, 256, 384)
-        quantize_g(1, 0, 256)
-        quantize_g(1, 256, SLOTS)
+        cast_pair(v, gb[1], g_raw[1][1], 1, 0, 0, 128)
+        cast_pair(s, gb[1], g_raw[1][1], 1, 0, 352, SLOTS)
+        cast_pair(v, gb[1], g_raw[1][1], 1, 0, 128, 352)
+        quantize_g(1, 0, 128)
+        quantize_g(1, 384, SLOTS)
+        quantize_g(1, 128, 384)
         cast_words(s, qb[0], q_raw[0], 0, 0, D)
         cast_words(v, qb[1], q_raw[1], 0, 0, 48)
         quantize_q(0)
@@ -133,6 +134,7 @@ def tile_attend_dk_kernel(tc, g, qm, offs, out):
         quantize_q(1)
         multiply(1)
 
-        nc.scalar.copy(sums[:], acc[:])
-        nc.vector.tensor_copy(placed[:].indirect(offsets[:]), sums[:])
+        for lo, hi in ((0, 128), (128, SLOTS)):
+            nc.scalar.copy(sums[:, lo:hi], acc[:, lo:hi])
+            nc.vector.tensor_copy(placed[:].indirect(offsets[:, lo // 16 : hi // 16]), sums[:, lo:hi])
         nc.sync.dma_start(out=out, in_=placed[:])

@@ -87,16 +87,15 @@ def tile_attend_dk_kernel(tc, g, qm, offs, out):
         q_raw = [load(qm_rows[c], f"q_raw{c}") for c in range(PASSES)]
         nc.sync.dma_start(offsets[:], offs)
 
-        nc.vector.memset(placed[:], 0.0)
-
         identity_bf16 = held.tile([P, P], BF16, name="identity_bf16")
         identity_f32 = held.tile([P, P], F32, name="identity_f32")
         make_identity(nc, identity_bf16[:])
         make_identity(nc, identity_f32[:])
+        nc.gpsimd.memset(placed[:], 0.0)
         spare_bf16 = [psum.tile([P, 4, P], BF16, name=f"spare_bf16{b}") for b in range(4)]
         spare_f32 = [psum.tile([P, SLOTS], F32, name=f"spare_f32{b}") for b in range(3)]
 
-        for i in range(32):
+        for i in range(40):
             nc.tensor.transpose(spare_bf16[i // 4 % 4][:, i % 4, :], identity_bf16[:], identity_bf16[:])
 
         def warm(raw, banks):
@@ -106,10 +105,9 @@ def tile_attend_dk_kernel(tc, g, qm, offs, out):
                 first = i % blocks * P
                 nc.tensor.transpose(banks[i // 4][:, i % 4 * P : (i % 4 + 1) * P], words[:, first : first + P], identity_f32[:])
 
-        warm(g_raw[0][1], spare_f32[:3])
         warm(g_raw[1][0], spare_f32[:3])
         warm(g_raw[1][1], spare_f32[:3])
-        warm(q_raw[0], [spare_f32[0], acc])
+        warm(q_raw[0], [acc])
 
         def cast_g(c, h, cut):
             cast_pair(v, gb[c], g_raw[c][h], h, 0, 0, cut)

@@ -91,7 +91,8 @@ def tile_attend_dk_kernel(tc, g, qm, offs, out):
         identity_f32 = held.tile([P, P], F32, name="identity_f32")
         make_identity(nc, identity_bf16[:])
         make_identity(nc, identity_f32[:])
-        nc.gpsimd.memset(placed[:], 0.0)
+        nc.vector.memset(placed[:, : TOKENS // 2 + 1], 0.0)
+        nc.vector.memset(placed[:, TOKENS // 2 + 1 :], 0.0)
         spare_bf16 = [psum.tile([P, 4, P], BF16, name=f"spare_bf16{b}") for b in range(4)]
         spare_f32 = [psum.tile([P, SLOTS], F32, name=f"spare_f32{b}") for b in range(3)]
 

@@ -30,12 +30,12 @@ def tile_attend_dk_kernel(tc, g, qm, offs, out):
         psum = ctx.enter_context(tc.psum_pool(name="psum", bufs=1))
 
         offsets = held.tile([P, SLOTS // 16], U16, name="offsets")
-        placed = held.tile([P, TOKENS], F32, name="placed")
+        placed = held.tile([P, TOKENS], F32, name="placed", align_bytes=256)
         sums = held.tile([P, SLOTS], F32, name="sums")
         acc = psum.tile([D, SLOTS], F32, name="acc")
 
         def load(rows, name):
-            raw = held.tile([P, rows.shape[1], rows.shape[2]], F32, name=name)
+            raw = held.tile([P, rows.shape[1], rows.shape[2]], F32, name=name, align_bytes=256)
             nc.sync.dma_start(out=raw[:], in_=rows)
             return raw
 

@@ -30,21 +30,21 @@ def tile_attend_dk_kernel(tc, g, qm, offs, out):
         psum = ctx.enter_context(tc.psum_pool(name="psum", bufs=1))
 
         offsets = held.tile([P, SLOTS // 16], U16, name="offsets")
-        placed = held.tile([P, TOKENS], F32, name="placed", align_bytes=256)
-        sums = held.tile([P, SLOTS], F32, name="sums")
+        placed = held.tile([P, TOKENS], F32, name="placed", align_bytes=4096)
+        sums = held.tile([P, SLOTS], F32, name="sums", align_bytes=256)
         acc = psum.tile([D, SLOTS], F32, name="acc")
 
         def load(rows, name):
-            raw = held.tile([P, rows.shape[1], rows.shape[2]], F32, name=name, align_bytes=256)
+            raw = held.tile([P, rows.shape[1], rows.shape[2]], F32, name=name, align_bytes=4096)
             nc.sync.dma_start(out=raw[:], in_=rows)
             return raw
 
-        g_codes = [held.tile([P, SLOTS], U32, name=f"g_codes{c}", align_bytes=64) for c in range(PASSES)]
-        g_scales = [held.tile([P, SLOTS], U8, name=f"g_scales{c}", align_bytes=64) for c in range(PASSES)]
-        q_codes = [held.tile([P, D], U32, name=f"q_codes{c}", align_bytes=64) for c in range(PASSES)]
-        q_scales = [held.tile([P, D], U8, name=f"q_scales{c}", align_bytes=64) for c in range(PASSES)]
-        gb = [held.tile([P, SLOTS, PACK], BF16, name=f"gb{c}", align_bytes=64) for c in range(PASSES)]
-        qb = [held.tile([P, D, PACK], BF16, name=f"qb{c}", align_bytes=64) for c in range(PASSES)]
+        g_codes = [held.tile([P, SLOTS], U32, name=f"g_codes{c}", align_bytes=256) for c in range(PASSES)]
+        g_scales = [held.tile([P, SLOTS], U8, name=f"g_scales{c}", align_bytes=256) for c in range(PASSES)]
+        q_codes = [held.tile([P, D], U32, name=f"q_codes{c}", align_bytes=256) for c in range(PASSES)]
+        q_scales = [held.tile([P, D], U8, name=f"q_scales{c}", align_bytes=256) for c in range(PASSES)]
+        gb = [held.tile([P, SLOTS, PACK], BF16, name=f"gb{c}", align_bytes=256) for c in range(PASSES)]
+        qb = [held.tile([P, D, PACK], BF16, name=f"qb{c}", align_bytes=256) for c in range(PASSES)]
         v, s = nc.vector.tensor_copy, nc.scalar.copy
 
         def quantize(grouped, codes, scales, lo, hi, dtype):

@@ -93,6 +93,9 @@ def tile_attend_dk_kernel(tc, g, qm, offs, out):
         make_identity(nc, identity_f32[:])
         nc.vector.memset(placed[:, : TOKENS // 2 + 1], 0.0)
         nc.vector.memset(placed[:, TOKENS // 2 + 1 :], 0.0)
+        zeros = held.tile([P, 96], F32, name="zeros", align_bytes=256)
+        nc.vector.memset(zeros[:, :49], 0.0)
+        nc.vector.memset(zeros[:, 49:], 0.0)
         spare_bf16 = [psum.tile([P, 4, P], BF16, name=f"spare_bf16{b}") for b in range(4)]
         spare_f32 = [psum.tile([P, SLOTS], F32, name=f"spare_f32{b}") for b in range(3)]
 
@@ -120,20 +123,22 @@ def tile_attend_dk_kernel(tc, g, qm, offs, out):
         quantize_g(0, 256, SLOTS)
         cast_g(1, 0, 256)
         cast_pair(v, gb[1], g_raw[1][1], 1, 0, 0, 128)
-        cast_pair(s, gb[1], g_raw[1][1], 1, 0, 352, SLOTS)
-        cast_pair(v, gb[1], g_raw[1][1], 1, 0, 128, 352)
+        cast_pair(s, gb[1], g_raw[1][1], 1, 0, 336, SLOTS)
+        cast_pair(v, gb[1], g_raw[1][1], 1, 0, 128, 256)
+        cast_pair(v, gb[1], g_raw[1][1], 1, 0, 256, 336)
         quantize_g(1, 0, 128)
-        quantize_g(1, 384, SLOTS)
-        quantize_g(1, 128, 384)
+        quantize_g(1, 128, 256)
+        quantize_g(1, 256, SLOTS)
         cast_words(s, qb[0], q_raw[0], 0, 0, D)
-        cast_words(v, qb[1], q_raw[1], 0, 0, 48)
+        cast_words(v, qb[1], q_raw[1], 0, 0, 40)
         quantize_q(0)
         multiply(0)
-        cast_words(s, qb[1], q_raw[1], 0, 48, D)
+        cast_words(s, qb[1], q_raw[1], 0, 40, D)
         quantize_q(1)
         multiply(1)
 
-        for lo, hi in ((0, 128), (128, SLOTS)):
-            nc.scalar.copy(sums[:, lo:hi], acc[:, lo:hi])
-            nc.vector.tensor_copy(placed[:].indirect(offsets[:, lo // 16 : hi // 16]), sums[:, lo:hi])
+        nc.scalar.copy(sums[:, :96], acc[:, :96])
+        nc.vector.tensor_tensor(placed[:].indirect(offsets[:, :6]), sums[:, :96], zeros[:], mybir.AluOpType.add)
+        nc.scalar.copy(sums[:, 96:], acc[:, 96:])
+        nc.vector.tensor_copy(placed[:].indirect(offsets[:, 6:]), sums[:, 96:])
         nc.sync.dma_start(out=out, in_=placed[:])

@@ -104,10 +104,9 @@ def tile_attend_dk_kernel(tc, g, qm, offs, out):
 
         def warm(raw, banks):
             words = raw[:].rearrange("p j w -> p (j w)")
-            blocks = words.shape[1] // P
             for i in range(4 * len(banks)):
-                first = i % blocks * P
-                nc.tensor.transpose(banks[i // 4][:, i % 4 * P : (i % 4 + 1) * P], words[:, first : first + P], identity_f32[:])
+                source = identity_f32[:] if i % 4 else words[:, :P]
+                nc.tensor.transpose(banks[i // 4][:, i % 4 * P : (i % 4 + 1) * P], source, identity_f32[:])
 
         warm(g_raw[1][0], spare_f32[:3])
         warm(g_raw[1][1], spare_f32[:3])

@@ -93,9 +93,9 @@ def tile_attend_dk_kernel(tc, g, qm, offs, out):
         make_identity(nc, identity_f32[:])
         nc.vector.memset(placed[:, : TOKENS // 2 + 1], 0.0)
         nc.vector.memset(placed[:, TOKENS // 2 + 1 :], 0.0)
-        zeros = held.tile([P, 96], F32, name="zeros", align_bytes=256)
-        nc.vector.memset(zeros[:, :49], 0.0)
-        nc.vector.memset(zeros[:, 49:], 0.0)
+        zeros = held.tile([P, 64], F32, name="zeros", align_bytes=256)
+        nc.vector.memset(zeros[:, :33], 0.0)
+        nc.vector.memset(zeros[:, 33:], 0.0)
         spare_bf16 = [psum.tile([P, 4, P], BF16, name=f"spare_bf16{b}") for b in range(4)]
         spare_f32 = [psum.tile([P, SLOTS], F32, name=f"spare_f32{b}") for b in range(3)]
 
@@ -136,8 +136,8 @@ def tile_attend_dk_kernel(tc, g, qm, offs, out):
         quantize_q(1)
         multiply(1)
 
-        nc.scalar.copy(sums[:, :96], acc[:, :96])
-        nc.vector.tensor_tensor(placed[:].indirect(offsets[:, :6]), sums[:, :96], zeros[:], mybir.AluOpType.add)
-        nc.scalar.copy(sums[:, 96:], acc[:, 96:])
-        nc.vector.tensor_copy(placed[:].indirect(offsets[:, 6:]), sums[:, 96:])
+        nc.scalar.copy(sums[:, :64], acc[:, :64])
+        nc.vector.tensor_tensor(placed[:].indirect(offsets[:, :4]), sums[:, :64], zeros[:], mybir.AluOpType.add)
+        nc.scalar.copy(sums[:, 64:], acc[:, 64:])
+        nc.vector.tensor_copy(placed[:].indirect(offsets[:, 4:]), sums[:, 64:])
         nc.sync.dma_start(out=out, in_=placed[:])

@@ -93,7 +93,7 @@ def tile_attend_dk_kernel(tc, g, qm, offs, out):
         make_identity(nc, identity_f32[:])
         nc.vector.memset(placed[:, : TOKENS // 2 + 1], 0.0)
         nc.vector.memset(placed[:, TOKENS // 2 + 1 :], 0.0)
-        zeros = held.tile([P, 64], F32, name="zeros", align_bytes=256)
+        zeros = held.tile([P, 448], F32, name="zeros", align_bytes=256)
         nc.vector.memset(zeros[:, :33], 0.0)
         nc.vector.memset(zeros[:, 33:], 0.0)
         spare_bf16 = [psum.tile([P, 4, P], BF16, name=f"spare_bf16{b}") for b in range(4)]
@@ -137,7 +137,7 @@ def tile_attend_dk_kernel(tc, g, qm, offs, out):
         multiply(1)
 
         nc.scalar.copy(sums[:, :64], acc[:, :64])
-        nc.vector.tensor_tensor(placed[:].indirect(offsets[:, :4]), sums[:, :64], zeros[:], mybir.AluOpType.add)
+        nc.vector.tensor_tensor(placed[:].indirect(offsets[:, :4]), sums[:, :64], zeros[:, :64], mybir.AluOpType.add)
         nc.scalar.copy(sums[:, 64:], acc[:, 64:])
-        nc.vector.tensor_copy(placed[:].indirect(offsets[:, 4:]), sums[:, 64:])
+        nc.vector.tensor_tensor(placed[:].indirect(offsets[:, 4:]), sums[:, 64:], zeros[:], mybir.AluOpType.add)
         nc.sync.dma_start(out=out, in_=placed[:])

@@ -1,7 +1,6 @@
 from contextlib import ExitStack
 
 import concourse.mybir as mybir
-from concourse.masks import make_identity
 
 Q, SLOTS, TOKENS, D = 1024, 512, 1024, 128
 
@@ -87,30 +86,11 @@ def tile_attend_dk_kernel(tc, g, qm, offs, out):
         q_raw = [load(qm_rows[c], f"q_raw{c}") for c in range(PASSES)]
         nc.sync.dma_start(offsets[:], offs)
 
-        identity_bf16 = held.tile([P, P], BF16, name="identity_bf16")
-        identity_f32 = held.tile([P, P], F32, name="identity_f32")
-        make_identity(nc, identity_bf16[:])
-        make_identity(nc, identity_f32[:])
         nc.vector.memset(placed[:, : TOKENS // 2 + 1], 0.0)
         nc.vector.memset(placed[:, TOKENS // 2 + 1 :], 0.0)
         zeros = held.tile([P, 448], F32, name="zeros", align_bytes=256)
         nc.vector.memset(zeros[:, :33], 0.0)
         nc.vector.memset(zeros[:, 33:], 0.0)
-        spare_bf16 = [psum.tile([P, 4, P], BF16, name=f"spare_bf16{b}") for b in range(4)]
-        spare_f32 = [psum.tile([P, SLOTS], F32, name=f"spare_f32{b}") for b in range(3)]
-
-        for i in range(40):
-            nc.tensor.transpose(spare_bf16[i // 4 % 4][:, i % 4, :], identity_bf16[:], identity_bf16[:])
-
-        def warm(raw, banks):
-            words = raw[:].rearrange("p j w -> p (j w)")
-            for i in range(4 * len(banks)):
-                source = identity_f32[:] if i % 4 else words[:, :P]
-                nc.tensor.transpose(banks[i // 4][:, i % 4 * P : (i % 4 + 1) * P], source, identity_f32[:])
-
-        warm(g_raw[1][0], spare_f32[:3])
-        warm(g_raw[1][1], spare_f32[:3])
-        warm(q_raw[0], [acc])
 
         def cast_g(c, h, cut):
             cast_pair(v, gb[c], g_raw[c][h], h, 0, 0, cut)

@@ -82,8 +82,10 @@ def tile_attend_dk_kernel(tc, g, qm, offs, out):
                 raw[:, :, lo:hi].rearrange("p j w -> p w j"),
             )
 
-        g_raw = [[load(g_rows[c][:, 2 * h : 2 * h + 2, :], f"g_raw{c}{h}") for h in range(2)] for c in range(PASSES)]
-        q_raw = [load(qm_rows[c], f"q_raw{c}") for c in range(PASSES)]
+        g_raw, q_raw = [], []
+        for c in range(PASSES):
+            g_raw.append([load(g_rows[c][:, 2 * h : 2 * h + 2, :], f"g_raw{c}{h}") for h in range(2)])
+            q_raw.append(load(qm_rows[c], f"q_raw{c}"))
         nc.sync.dma_start(offsets[:], offs)
 
         nc.vector.memset(placed[:, : TOKENS // 2 + 1], 0.0)
@@ -100,19 +102,18 @@ def tile_attend_dk_kernel(tc, g, qm, offs, out):
         cast_g(0, 1, 256)
         quantize_g(0, 0, 256)
         quantize_g(0, 256, SLOTS)
+        cast_words(s, qb[0], q_raw[0], 0, 0, D)
+        quantize_q(0)
+        multiply(0)
         cast_g(1, 0, 256)
         cast_pair(v, gb[1], g_raw[1][1], 1, 0, 0, 128)
-        cast_pair(s, gb[1], g_raw[1][1], 1, 0, 336, SLOTS)
+        cast_pair(s, gb[1], g_raw[1][1], 1, 0, 352, SLOTS)
         cast_pair(v, gb[1], g_raw[1][1], 1, 0, 128, 256)
-        cast_pair(v, gb[1], g_raw[1][1], 1, 0, 256, 336)
+        cast_pair(v, gb[1], g_raw[1][1], 1, 0, 256, 352)
         quantize_g(1, 0, 128)
         quantize_g(1, 128, 256)
         quantize_g(1, 256, SLOTS)
-        cast_words(s, qb[0], q_raw[0], 0, 0, D)
-        cast_words(v, qb[1], q_raw[1], 0, 0, 40)
-        quantize_q(0)
-        multiply(0)
-        cast_words(s, qb[1], q_raw[1], 0, 40, D)
+        cast_words(s, qb[1], q_raw[1], 0, 0, D)
         quantize_q(1)
         multiply(1)
 

@@ -88,11 +88,9 @@ def tile_attend_dk_kernel(tc, g, qm, offs, out):
             q_raw.append(load(qm_rows[c], f"q_raw{c}"))
         nc.sync.dma_start(offsets[:], offs)
 
-        nc.vector.memset(placed[:, : TOKENS // 2 + 1], 0.0)
-        nc.vector.memset(placed[:, TOKENS // 2 + 1 :], 0.0)
+        nc.vector.memset(placed[:], 0.0)
         zeros = held.tile([P, 448], F32, name="zeros", align_bytes=256)
-        nc.vector.memset(zeros[:, :33], 0.0)
-        nc.vector.memset(zeros[:, 33:], 0.0)
+        nc.vector.memset(zeros[:], 0.0)
 
         def cast_g(c, h, cut):
             cast_pair(v, gb[c], g_raw[c][h], h, 0, 0, cut)
@@ -113,8 +111,9 @@ def tile_attend_dk_kernel(tc, g, qm, offs, out):
         quantize_g(1, 0, 128)
         quantize_g(1, 128, 256)
         quantize_g(1, 256, SLOTS)
-        cast_words(s, qb[1], q_raw[1], 0, 0, D)
-        quantize_q(1)
+        for lo in (0, D // 2):
+            cast_words(s, qb[1], q_raw[1], 0, lo, lo + D // 2)
+            quantize(qb[1], q_codes[1], q_scales[1], lo, lo + D // 2, E4M3X4)
         multiply(1)
 
         nc.scalar.copy(sums[:, :64], acc[:, :64])

@@ -82,10 +82,15 @@ def tile_attend_dk_kernel(tc, g, qm, offs, out):
                 raw[:, :, lo:hi].rearrange("p j w -> p w j"),
             )
 
-        g_raw, q_raw = [], []
-        for c in range(PASSES):
-            g_raw.append([load(g_rows[c][:, 2 * h : 2 * h + 2, :], f"g_raw{c}{h}") for h in range(2)])
-            q_raw.append(load(qm_rows[c], f"q_raw{c}"))
+        g_raw = [[load(g_rows[0][:, 2 * h : 2 * h + 2, :], f"g_raw0{h}") for h in range(2)]]
+        q_raw = [load(qm_rows[0], "q_raw0")]
+        last = held.tile([P, PACK * SLOTS], F32, name="g_raw1", align_bytes=4096)
+        last_rows = g_rows[1].rearrange("p j n -> p (j n)")
+        early = (PACK - 1) * SLOTS + 192
+        nc.sync.dma_start(out=last[:, :early], in_=last_rows[:, :early])
+        nc.sync.dma_start(out=last[:, early:], in_=last_rows[:, early:])
+        last_raw = last[:].rearrange("p (j n) -> p j n", j=PACK)
+        q_raw.append(load(qm_rows[1], "q_raw1"))
         nc.sync.dma_start(offsets[:], offs)
 
         nc.vector.memset(placed[:], 0.0)
@@ -103,16 +108,17 @@ def tile_attend_dk_kernel(tc, g, qm, offs, out):
         cast_words(s, qb[0], q_raw[0], 0, 0, D)
         quantize_q(0)
         multiply(0)
-        cast_g(1, 0, 256)
-        cast_pair(v, gb[1], g_raw[1][1], 1, 0, 0, 128)
-        cast_pair(s, gb[1], g_raw[1][1], 1, 0, 352, SLOTS)
-        cast_pair(v, gb[1], g_raw[1][1], 1, 0, 128, 256)
-        cast_pair(v, gb[1], g_raw[1][1], 1, 0, 256, 352)
-        quantize_g(1, 0, 128)
-        quantize_g(1, 128, 256)
-        quantize_g(1, 256, SLOTS)
+        cast_words(v, gb[1], last_raw, 0, 0, 128)
+        cast_words(s, gb[1], last_raw, 0, 128, 192)
+        cast_words(v, gb[1], last_raw, 0, 192, 256)
+        cast_words(v, gb[1], last_raw, 0, 256, 368)
+        cast_words(s, gb[1], last_raw, 0, 368, SLOTS)
+        quantize_g(1, 0, 256)
+        cast_words(s, qb[1], q_raw[1], 0, 0, D // 2)
+        cast_words(v, qb[1], q_raw[1], 0, D // 2, D)
+        quantize_g(1, 256, 384)
+        quantize_g(1, 384, SLOTS)
         for lo in (0, D // 2):
-            cast_words(s, qb[1], q_raw[1], 0, lo, lo + D // 2)
             quantize(qb[1], q_codes[1], q_scales[1], lo, lo + D // 2, E4M3X4)
         multiply(1)
 

@@ -111,13 +111,13 @@ def tile_attend_dk_kernel(tc, g, qm, offs, out):
         cast_words(v, gb[1], last_raw, 0, 0, 128)
         cast_words(s, gb[1], last_raw, 0, 128, 192)
         cast_words(v, gb[1], last_raw, 0, 192, 256)
-        cast_words(v, gb[1], last_raw, 0, 256, 368)
-        cast_words(s, gb[1], last_raw, 0, 368, SLOTS)
+        cast_words(v, gb[1], last_raw, 0, 256, 384)
+        cast_words(s, gb[1], last_raw, 0, 384, SLOTS)
         quantize_g(1, 0, 256)
         cast_words(s, qb[1], q_raw[1], 0, 0, D // 2)
-        cast_words(v, qb[1], q_raw[1], 0, D // 2, D)
-        quantize_g(1, 256, 384)
-        quantize_g(1, 384, SLOTS)
+        cast_words(v, qb[1], q_raw[1], 0, 88, D)
+        cast_words(s, qb[1], q_raw[1], 0, D // 2, 88)
+        quantize_g(1, 256, SLOTS)
         for lo in (0, D // 2):
             quantize(qb[1], q_codes[1], q_scales[1], lo, lo + D // 2, E4M3X4)
         multiply(1)

@@ -17,21 +17,23 @@ E5M2X4 = mybir.dt.float8_e5m2_x4
 P = 128
 PACK = 4
 PASSES = Q // (P * PACK)
+GROUP = 128
+GROUPS = SLOTS // GROUP
 
 
 def tile_attend_dk_kernel(tc, g, qm, offs, out):
     nc = tc.nc
     g_rows = g.rearrange("b (c p j) n -> (b c) p j n", p=P, j=PACK)
-    qm_rows = qm.rearrange("b (c p j) d -> (b c) p j d", p=P, j=PACK)
+    qm_rows = qm.rearrange("b (c p j) d -> p (b c) (j d)", p=P, j=PACK)
 
     with ExitStack() as ctx:
         held = ctx.enter_context(tc.tile_pool(name="held", bufs=1))
         psum = ctx.enter_context(tc.psum_pool(name="psum", bufs=1))
 
         offsets = held.tile([P, SLOTS // 16], U16, name="offsets")
-        placed = held.tile([P, TOKENS], F32, name="placed", align_bytes=4096)
+        low = held.tile([P, TOKENS], F32, name="low", align_bytes=4096)
         sums = held.tile([P, SLOTS], F32, name="sums", align_bytes=256)
-        acc = psum.tile([D, SLOTS], F32, name="acc")
+        acc = [psum.tile([D, GROUP], F32, name=f"acc{k}") for k in range(GROUPS)]
 
         def load(rows, name):
             raw = held.tile([P, rows.shape[1], rows.shape[2]], F32, name=name, align_bytes=4096)
@@ -59,71 +61,72 @@ def tile_attend_dk_kernel(tc, g, qm, offs, out):
         def quantize_q(c):
             quantize(qb[c], q_codes[c], q_scales[c], 0, D, E4M3X4)
 
-        def multiply(c):
+        def multiply(c, k):
+            cols = slice(k * GROUP, (k + 1) * GROUP)
             nc.tensor.matmul_mx(
-                out=acc[:],
+                out=acc[k][:],
                 lhsT=q_codes[c][:].bitcast(E4M3X4),
                 lhsT_scale=q_scales[c][:],
-                rhs=g_codes[c][:].bitcast(E5M2X4),
-                rhs_scale=g_scales[c][:],
+                rhs=g_codes[c][:, cols].bitcast(E5M2X4),
+                rhs_scale=g_scales[c][:, cols],
                 start=(c == 0),
                 stop=(c == PASSES - 1),
             )
 
-        def cast_words(copy, grouped, raw, first, lo, hi):
+        def cast_words(copy, grouped, raw):
             copy(
-                grouped[:, first + lo : first + hi, :].rearrange("p (b i) j -> p b j i", i=4),
-                raw[:, :, lo:hi].rearrange("p j (b i) -> p b j i", i=4),
+                grouped[:].rearrange("p (b i) j -> p b j i", i=4),
+                raw.rearrange("p (j b i) -> p b j i", j=PACK, i=4),
             )
 
-        def cast_pair(copy, grouped, raw, h, first, lo, hi):
+        def cast_pair(copy, c, raw, h, first, lo, hi):
             copy(
-                grouped[:, first + lo : first + hi, 2 * h : 2 * h + 2],
-                raw[:, :, lo:hi].rearrange("p j w -> p w j"),
+                gb[c][:, lo:hi, 2 * h : 2 * h + 2],
+                raw[:, :, lo - first : hi - first].rearrange("p j w -> p w j"),
             )
 
-        g_raw = [[load(g_rows[0][:, 2 * h : 2 * h + 2, :], f"g_raw0{h}") for h in range(2)]]
-        q_raw = [load(qm_rows[0], "q_raw0")]
-        last = held.tile([P, PACK * SLOTS], F32, name="g_raw1", align_bytes=4096)
-        last_rows = g_rows[1].rearrange("p j n -> p (j n)")
-        early = (PACK - 1) * SLOTS + 192
-        nc.sync.dma_start(out=last[:, :early], in_=last_rows[:, :early])
-        nc.sync.dma_start(out=last[:, early:], in_=last_rows[:, early:])
-        last_raw = last[:].rearrange("p (j n) -> p j n", j=PACK)
-        q_raw.append(load(qm_rows[1], "q_raw1"))
+        def copy_out(copy, k):
+            copy(sums[:, k * GROUP : (k + 1) * GROUP], acc[k][:])
+
+        half = SLOTS // 2
+        g0 = [load(g_rows[0][:, 2 * h : 2 * h + 2, :], f"g_raw0{h}") for h in range(2)]
+        q_raw = load(qm_rows, "q_raw")
+        g1_first = load(g_rows[1][:, 0:2, :], "g_raw10")
+        g1_low = load(g_rows[1][:, 2:4, :half], "g_raw11_low")
+        g1_high = load(g_rows[1][:, 2:4, half:], "g_raw11_high")
         nc.sync.dma_start(offsets[:], offs)
 
-        nc.vector.memset(placed[:], 0.0)
-        zeros = held.tile([P, 448], F32, name="zeros", align_bytes=256)
-        nc.vector.memset(zeros[:], 0.0)
+        nc.vector.memset(low[:], 0.0)
 
-        def cast_g(c, h, cut):
-            cast_pair(v, gb[c], g_raw[c][h], h, 0, 0, cut)
-            cast_pair(s, gb[c], g_raw[c][h], h, 0, cut, SLOTS)
-
-        cast_g(0, 0, 256)
-        cast_g(0, 1, 256)
+        for h in range(2):
+            cast_pair(v, 0, g0[h], h, 0, 0, 256)
+            cast_pair(s, 0, g0[h], h, 0, 256, SLOTS)
         quantize_g(0, 0, 256)
         quantize_g(0, 256, SLOTS)
-        cast_words(s, qb[0], q_raw[0], 0, 0, D)
+        cast_words(s, qb[0], q_raw[:, 0, :])
+        cast_words(v, qb[1], q_raw[:, 1, :])
         quantize_q(0)
-        multiply(0)
-        cast_words(v, gb[1], last_raw, 0, 0, 128)
-        cast_words(s, gb[1], last_raw, 0, 128, 192)
-        cast_words(v, gb[1], last_raw, 0, 192, 256)
-        cast_words(v, gb[1], last_raw, 0, 256, 384)
-        cast_words(s, gb[1], last_raw, 0, 384, SLOTS)
-        quantize_g(1, 0, 256)
-        cast_words(s, qb[1], q_raw[1], 0, 0, D // 2)
-        cast_words(v, qb[1], q_raw[1], 0, 88, D)
-        cast_words(s, qb[1], q_raw[1], 0, D // 2, 88)
-        quantize_g(1, 256, SLOTS)
-        for lo in (0, D // 2):
-            quantize(qb[1], q_codes[1], q_scales[1], lo, lo + D // 2, E4M3X4)
-        multiply(1)
+        quantize_q(1)
+        for k in range(GROUPS):
+            multiply(0, k)
 
-        nc.scalar.copy(sums[:, :64], acc[:, :64])
-        nc.vector.tensor_tensor(placed[:].indirect(offsets[:, :4]), sums[:, :64], zeros[:, :64], mybir.AluOpType.add)
-        nc.scalar.copy(sums[:, 64:], acc[:, 64:])
-        nc.vector.tensor_tensor(placed[:].indirect(offsets[:, 4:]), sums[:, 64:], zeros[:], mybir.AluOpType.add)
-        nc.sync.dma_start(out=out, in_=placed[:])
+        cast_pair(v, 1, g1_first, 0, 0, 0, 352)
+        cast_pair(s, 1, g1_first, 0, 0, 352, SLOTS)
+        cast_pair(s, 1, g1_low, 1, 0, 0, 128)
+        cast_pair(v, 1, g1_low, 1, 0, 128, 256)
+        quantize_g(1, 0, 128)
+        quantize_g(1, 128, 256)
+        multiply(1, 0)
+        multiply(1, 1)
+        cast_pair(s, 1, g1_high, 1, half, 256, 384)
+        cast_pair(v, 1, g1_high, 1, half, 384, SLOTS)
+        quantize_g(1, 256, 384)
+        quantize_g(1, 384, SLOTS)
+        multiply(1, 2)
+        multiply(1, 3)
+
+        for k in range(GROUPS):
+            copy_out(s, k)
+        for lo in (0, half):
+            nc.vector.tensor_copy(low[:].indirect(offsets[:, lo // 16 : (lo + half) // 16]), sums[:, lo : lo + half])
+        nc.sync.dma_start(out=out, in_=low[:])

@@ -32,7 +32,6 @@ def tile_attend_dk_kernel(tc, g, qm, offs, out):
 
         offsets = held.tile([P, SLOTS // 16], U16, name="offsets")
         low = held.tile([P, TOKENS], F32, name="low", align_bytes=4096)
-        sums = held.tile([P, SLOTS], F32, name="sums", align_bytes=256)
         acc = [psum.tile([D, GROUP], F32, name=f"acc{k}") for k in range(GROUPS)]
 
         def load(rows, name):
@@ -75,8 +74,8 @@ def tile_attend_dk_kernel(tc, g, qm, offs, out):
 
         def cast_words(copy, grouped, raw):
             copy(
-                grouped[:].rearrange("p (b i) j -> p b j i", i=4),
-                raw.rearrange("p (j b i) -> p b j i", j=PACK, i=4),
+                grouped.rearrange("p (b i) j -> p b j i", i=4),
+                raw.rearrange("p j (b i) -> p b j i", i=4),
             )
 
         def cast_pair(copy, c, raw, h, first, lo, hi):
@@ -91,9 +90,13 @@ def tile_attend_dk_kernel(tc, g, qm, offs, out):
         half = SLOTS // 2
         g0 = [load(g_rows[0][:, 2 * h : 2 * h + 2, :], f"g_raw0{h}") for h in range(2)]
         q_raw = load(qm_rows, "q_raw")
-        g1_first = load(g_rows[1][:, 0:2, :], "g_raw10")
-        g1_low = load(g_rows[1][:, 2:4, :half], "g_raw11_low")
-        g1_high = load(g_rows[1][:, 2:4, half:], "g_raw11_high")
+        last = held.tile([P, PACK * SLOTS], F32, name="g_raw1", align_bytes=4096)
+        g1 = last[:].rearrange("p (j n) -> p j n", j=PACK)
+        early = SLOTS + half
+        nc.sync.dma_start(out=last[:, :early], in_=g_rows[1].rearrange("p j n -> p (j n)")[:, :early])
+        nc.sync.dma_start(out=g1[:, 2:, :half], in_=g_rows[1][:, 2:, :half])
+        nc.sync.dma_start(out=g1[:, 1:, half:], in_=g_rows[1][:, 1:, half:])
+        sums = last[:, 2 * SLOTS - GROUP : 3 * SLOTS - GROUP]
         nc.sync.dma_start(offsets[:], offs)
 
         nc.vector.memset(low[:], 0.0)
@@ -103,27 +106,26 @@ def tile_attend_dk_kernel(tc, g, qm, offs, out):
             cast_pair(s, 0, g0[h], h, 0, 256, SLOTS)
         quantize_g(0, 0, 256)
         quantize_g(0, 256, SLOTS)
-        cast_words(s, qb[0], q_raw[:, 0, :])
-        cast_words(v, qb[1], q_raw[:, 1, :])
+        cast_words(v, qb[0][:], q_raw[:, 0, :].rearrange("p (j d) -> p j d", j=PACK))
+        cast_words(s, qb[1][:], q_raw[:, 1, :].rearrange("p (j d) -> p j d", j=PACK))
         quantize_q(0)
-        quantize_q(1)
         for k in range(GROUPS):
             multiply(0, k)
+        quantize_q(1)
 
-        cast_pair(v, 1, g1_first, 0, 0, 0, 352)
-        cast_pair(s, 1, g1_first, 0, 0, 352, SLOTS)
-        cast_pair(s, 1, g1_low, 1, 0, 0, 128)
-        cast_pair(v, 1, g1_low, 1, 0, 128, 256)
-        quantize_g(1, 0, 128)
-        quantize_g(1, 128, 256)
-        multiply(1, 0)
-        multiply(1, 1)
-        cast_pair(s, 1, g1_high, 1, half, 256, 384)
-        cast_pair(v, 1, g1_high, 1, half, 384, SLOTS)
-        quantize_g(1, 256, 384)
-        quantize_g(1, 384, SLOTS)
-        multiply(1, 2)
-        multiply(1, 3)
+        cast_pair(v, 1, g1[:, :2, :], 0, 0, 0, 160)
+        cast_pair(s, 1, g1[:, :2, :], 0, 0, 160, half)
+        for k in (0, 1):
+            cast_pair(v, 1, g1[:, 2:, :], 1, 0, k * GROUP, (k + 1) * GROUP)
+        for k in (0, 1):
+            quantize_g(1, k * GROUP, (k + 1) * GROUP)
+            multiply(1, k)
+        cast_words(v, gb[1][:, half:384, :], g1[:, :, half:384])
+        cast_pair(s, 1, g1[:, :2, :], 0, 0, 384, SLOTS)
+        cast_pair(v, 1, g1[:, 2:, :], 1, 0, 384, SLOTS)
+        for k in (2, 3):
+            quantize_g(1, k * GROUP, (k + 1) * GROUP)
+            multiply(1, k)
 
         for k in range(GROUPS):
             copy_out(s, k)

@@ -13,12 +13,14 @@ U16 = mybir.dt.uint16
 U8 = mybir.dt.uint8
 E4M3X4 = mybir.dt.float8_e4m3fn_x4
 E5M2X4 = mybir.dt.float8_e5m2_x4
+COPY = mybir.ActivationFunctionType.Copy
 
 P = 128
 PACK = 4
 PASSES = Q // (P * PACK)
 GROUP = 128
 GROUPS = SLOTS // GROUP
+HEAD = 288
 
 
 def tile_attend_dk_kernel(tc, g, qm, offs, out):
@@ -32,6 +34,7 @@ def tile_attend_dk_kernel(tc, g, qm, offs, out):
 
         offsets = held.tile([P, SLOTS // 16], U16, name="offsets")
         low = held.tile([P, TOKENS], F32, name="low", align_bytes=4096)
+        head = held.tile([P, TOKENS], F32, name="head", align_bytes=4096)
         acc = [psum.tile([D, GROUP], F32, name=f"acc{k}") for k in range(GROUPS)]
 
         def load(rows, name):
@@ -88,47 +91,50 @@ def tile_attend_dk_kernel(tc, g, qm, offs, out):
             copy(sums[:, k * GROUP : (k + 1) * GROUP], acc[k][:])
 
         half = SLOTS // 2
-        g0 = [load(g_rows[0][:, 2 * h : 2 * h + 2, :], f"g_raw0{h}") for h in range(2)]
         q_raw = load(qm_rows, "q_raw")
+        g0 = load(g_rows[0], "g_raw0")
         last = held.tile([P, PACK * SLOTS], F32, name="g_raw1", align_bytes=4096)
         g1 = last[:].rearrange("p (j n) -> p j n", j=PACK)
         early = SLOTS + half
         nc.sync.dma_start(out=last[:, :early], in_=g_rows[1].rearrange("p j n -> p (j n)")[:, :early])
         nc.sync.dma_start(out=g1[:, 2:, :half], in_=g_rows[1][:, 2:, :half])
         nc.sync.dma_start(out=g1[:, 1:, half:], in_=g_rows[1][:, 1:, half:])
-        sums = last[:, 2 * SLOTS - GROUP : 3 * SLOTS - GROUP]
+        sums = last[:, 2 * SLOTS - 32 : 3 * SLOTS - 32]
         nc.sync.dma_start(offsets[:], offs)
 
-        nc.vector.memset(low[:], 0.0)
+        nc.vector.memset(low[:, HEAD:], 0.0)
+        nc.vector.memset(head[:, :HEAD], 0.0)
 
-        for h in range(2):
-            cast_pair(v, 0, g0[h], h, 0, 0, 256)
-            cast_pair(s, 0, g0[h], h, 0, 256, SLOTS)
-        quantize_g(0, 0, 256)
-        quantize_g(0, 256, SLOTS)
-        cast_words(v, qb[0][:], q_raw[:, 0, :].rearrange("p (j d) -> p j d", j=PACK))
-        cast_words(s, qb[1][:], q_raw[:, 1, :].rearrange("p (j d) -> p j d", j=PACK))
-        quantize_q(0)
-        for k in range(GROUPS):
-            multiply(0, k)
+        for c, copy in ((0, s), (1, v)):
+            cast_words(copy, qb[c][:], q_raw[:, c, :].rearrange("p (j d) -> p j d", j=PACK))
         quantize_q(1)
+        quantize_q(0)
+        for copy, lo, hi in ((v, 0, half), (v, half, 320), (s, 320, SLOTS)):
+            cast_words(copy, gb[0][:, lo:hi, :], g0[:, :, lo:hi])
+        for lo in (0, half):
+            quantize_g(0, lo, lo + half)
+            multiply(0, lo // GROUP)
+            multiply(0, lo // GROUP + 1)
 
-        cast_pair(v, 1, g1[:, :2, :], 0, 0, 0, 160)
-        cast_pair(s, 1, g1[:, :2, :], 0, 0, 160, half)
+        cast_pair(s, 1, g1[:, :2, :], 0, 0, 0, half)
         for k in (0, 1):
             cast_pair(v, 1, g1[:, 2:, :], 1, 0, k * GROUP, (k + 1) * GROUP)
         for k in (0, 1):
             quantize_g(1, k * GROUP, (k + 1) * GROUP)
             multiply(1, k)
-        cast_words(v, gb[1][:, half:384, :], g1[:, :, half:384])
-        cast_pair(s, 1, g1[:, :2, :], 0, 0, 384, SLOTS)
-        cast_pair(v, 1, g1[:, 2:, :], 1, 0, 384, SLOTS)
+        for copy, lo, hi in ((v, half, 384), (v, 384, 480), (s, 480, SLOTS)):
+            cast_words(copy, gb[1][:, lo:hi, :], g1[:, :, lo:hi])
         for k in (2, 3):
             quantize_g(1, k * GROUP, (k + 1) * GROUP)
             multiply(1, k)
 
-        for k in range(GROUPS):
-            copy_out(s, k)
+        copy_out(s, 0)
+        copy_out(s, 1)
+        nc.scalar.activation(head[:].indirect(offsets[:, : GROUP // 16]), sums[:, :GROUP], COPY)
+        copy_out(s, 2)
+        copy_out(s, 3)
+        nc.scalar.activation(head[:].indirect(offsets[:, GROUP // 16 : HEAD // 16]), sums[:, GROUP:HEAD], COPY)
         for lo in (0, half):
             nc.vector.tensor_copy(low[:].indirect(offsets[:, lo // 16 : (lo + half) // 16]), sums[:, lo : lo + half])
-        nc.sync.dma_start(out=out, in_=low[:])
+        for window, cols in ((head, slice(0, HEAD)), (low, slice(HEAD, TOKENS))):
+            nc.sync.dma_start(out=out[:, cols], in_=window[:, cols])

@@ -109,20 +109,20 @@ def tile_attend_dk_kernel(tc, g, qm, offs, out):
             cast_words(copy, qb[c][:], q_raw[:, c, :].rearrange("p (j d) -> p j d", j=PACK))
         quantize_q(1)
         quantize_q(0)
-        for copy, lo, hi in ((v, 0, half), (v, half, 320), (s, 320, SLOTS)):
+        for copy, lo, hi in ((v, 0, GROUP), (v, GROUP, half), (v, half, 304), (s, 304, 384), (s, 384, SLOTS)):
             cast_words(copy, gb[0][:, lo:hi, :], g0[:, :, lo:hi])
-        for lo in (0, half):
-            quantize_g(0, lo, lo + half)
-            multiply(0, lo // GROUP)
-            multiply(0, lo // GROUP + 1)
+        for k in range(GROUPS):
+            quantize_g(0, k * GROUP, (k + 1) * GROUP)
+            multiply(0, k)
 
-        cast_pair(s, 1, g1[:, :2, :], 0, 0, 0, half)
-        for k in (0, 1):
-            cast_pair(v, 1, g1[:, 2:, :], 1, 0, k * GROUP, (k + 1) * GROUP)
+        cast_pair(s, 1, g1[:, :2, :], 0, 0, 0, GROUP)
+        cast_pair(v, 1, g1[:, 2:, :], 1, 0, 0, GROUP)
+        for copy, lo, hi in ((v, GROUP, 216), (s, 216, half)):
+            cast_words(copy, gb[1][:, lo:hi, :], g1[:, :, lo:hi])
         for k in (0, 1):
             quantize_g(1, k * GROUP, (k + 1) * GROUP)
             multiply(1, k)
-        for copy, lo, hi in ((v, half, 384), (v, 384, 480), (s, 480, SLOTS)):
+        for copy, lo, hi in ((v, half, 384), (v, 384, 448), (s, 480, SLOTS), (s, 448, 480)):
             cast_words(copy, gb[1][:, lo:hi, :], g1[:, :, lo:hi])
         for k in (2, 3):
             quantize_g(1, k * GROUP, (k + 1) * GROUP)

@@ -20,7 +20,7 @@ PACK = 4
 PASSES = Q // (P * PACK)
 GROUP = 128
 GROUPS = SLOTS // GROUP
-HEAD = 288
+HEAD = 320
 
 
 def tile_attend_dk_kernel(tc, g, qm, offs, out):
@@ -99,7 +99,7 @@ def tile_attend_dk_kernel(tc, g, qm, offs, out):
         nc.sync.dma_start(out=last[:, :early], in_=g_rows[1].rearrange("p j n -> p (j n)")[:, :early])
         nc.sync.dma_start(out=g1[:, 2:, :half], in_=g_rows[1][:, 2:, :half])
         nc.sync.dma_start(out=g1[:, 1:, half:], in_=g_rows[1][:, 1:, half:])
-        sums = last[:, 2 * SLOTS - 32 : 3 * SLOTS - 32]
+        sums = last[:, 2 * SLOTS - 16 : 3 * SLOTS - 16]
         nc.sync.dma_start(offsets[:], offs)
 
         nc.vector.memset(low[:, HEAD:], 0.0)
@@ -116,13 +116,14 @@ def tile_attend_dk_kernel(tc, g, qm, offs, out):
             multiply(0, k)
 
         cast_pair(s, 1, g1[:, :2, :], 0, 0, 0, GROUP)
-        cast_pair(v, 1, g1[:, 2:, :], 1, 0, 0, GROUP)
+        cast_pair(v, 1, g1[:, 2:, :], 1, 0, 0, 96)
+        cast_pair(s, 1, g1[:, 2:, :], 1, 0, 96, GROUP)
         for copy, lo, hi in ((v, GROUP, 216), (s, 216, half)):
             cast_words(copy, gb[1][:, lo:hi, :], g1[:, :, lo:hi])
         for k in (0, 1):
             quantize_g(1, k * GROUP, (k + 1) * GROUP)
             multiply(1, k)
-        for copy, lo, hi in ((v, half, 384), (v, 384, 448), (s, 480, SLOTS), (s, 448, 480)):
+        for copy, lo, hi in ((v, half, 384), (v, 384, 448), (s, 496, SLOTS), (s, 448, 496)):
             cast_words(copy, gb[1][:, lo:hi, :], g1[:, :, lo:hi])
         for k in (2, 3):
             quantize_g(1, k * GROUP, (k + 1) * GROUP)

@@ -123,7 +123,7 @@ def tile_attend_dk_kernel(tc, g, qm, offs, out):
         for k in (0, 1):
             quantize_g(1, k * GROUP, (k + 1) * GROUP)
             multiply(1, k)
-        for copy, lo, hi in ((v, half, 384), (v, 384, 448), (s, 496, SLOTS), (s, 448, 496)):
+        for copy, lo, hi in ((v, half, 352), (v, 384, 464), (s, 496, SLOTS), (s, 352, 384), (s, 464, 496)):
             cast_words(copy, gb[1][:, lo:hi, :], g1[:, :, lo:hi])
         for k in (2, 3):
             quantize_g(1, k * GROUP, (k + 1) * GROUP)

@@ -20,7 +20,11 @@ PACK = 4
 PASSES = Q // (P * PACK)
 GROUP = 128
 GROUPS = SLOTS // GROUP
+HALF = SLOTS // 2
 HEAD = 320
+LOW_EARLY_ON_VECTOR = 64
+LATE_ON_VECTOR = 88
+HIGH_EARLY_ON_SCALAR = 192
 
 
 def tile_attend_dk_kernel(tc, g, qm, offs, out):
@@ -33,21 +37,21 @@ def tile_attend_dk_kernel(tc, g, qm, offs, out):
         psum = ctx.enter_context(tc.psum_pool(name="psum", bufs=1))
 
         offsets = held.tile([P, SLOTS // 16], U16, name="offsets")
-        low = held.tile([P, TOKENS], F32, name="low", align_bytes=4096)
+        main = held.tile([P, TOKENS], F32, name="main", align_bytes=4096)
         head = held.tile([P, TOKENS], F32, name="head", align_bytes=4096)
         acc = [psum.tile([D, GROUP], F32, name=f"acc{k}") for k in range(GROUPS)]
 
-        def load(rows, name):
-            raw = held.tile([P, rows.shape[1], rows.shape[2]], F32, name=name, align_bytes=4096)
-            nc.sync.dma_start(out=raw[:], in_=rows)
-            return raw
-
         g_codes = [held.tile([P, SLOTS], U32, name=f"g_codes{c}", align_bytes=256) for c in range(PASSES)]
         g_scales = [held.tile([P, SLOTS], U8, name=f"g_scales{c}", align_bytes=256) for c in range(PASSES)]
-        q_codes = [held.tile([P, D], U32, name=f"q_codes{c}", align_bytes=256) for c in range(PASSES)]
-        q_scales = [held.tile([P, D], U8, name=f"q_scales{c}", align_bytes=256) for c in range(PASSES)]
+        q_codes = held.tile([P, PASSES * D], U32, name="q_codes", align_bytes=256)
+        q_scales = held.tile([P, PASSES * D], U8, name="q_scales", align_bytes=256)
         gb = [held.tile([P, SLOTS, PACK], BF16, name=f"gb{c}", align_bytes=256) for c in range(PASSES)]
-        qb = [held.tile([P, D, PACK], BF16, name=f"qb{c}", align_bytes=256) for c in range(PASSES)]
+        qb = held.tile([P, PASSES * D, PACK], BF16, name="qb", align_bytes=256)
+        g0 = held.tile([P, PACK, SLOTS], F32, name="g_raw0", align_bytes=4096)
+        q_raw = held.tile([P, PASSES, PACK * D], F32, name="q_raw", align_bytes=4096)
+        last = held.tile([P, PACK * SLOTS], F32, name="g_raw1", align_bytes=4096)
+        g1 = last[:].rearrange("p (j n) -> p j n", j=PACK)
+        g1_run = g_rows[1].rearrange("p j n -> p (j n)")
         v, s = nc.vector.tensor_copy, nc.scalar.copy
 
         def quantize(grouped, codes, scales, lo, hi, dtype):
@@ -57,18 +61,16 @@ def tile_attend_dk_kernel(tc, g, qm, offs, out):
                 in_=grouped[:, lo:hi, :].rearrange("p w j -> p (w j)"),
             )
 
-        def quantize_g(c, lo, hi):
-            quantize(gb[c], g_codes[c], g_scales[c], lo, hi, E5M2X4)
-
-        def quantize_q(c):
-            quantize(qb[c], q_codes[c], q_scales[c], 0, D, E4M3X4)
+        def quantize_g(c, k):
+            quantize(gb[c], g_codes[c], g_scales[c], k * GROUP, (k + 1) * GROUP, E5M2X4)
 
         def multiply(c, k):
             cols = slice(k * GROUP, (k + 1) * GROUP)
+            features = slice(c * D, (c + 1) * D)
             nc.tensor.matmul_mx(
                 out=acc[k][:],
-                lhsT=q_codes[c][:].bitcast(E4M3X4),
-                lhsT_scale=q_scales[c][:],
+                lhsT=q_codes[:, features].bitcast(E4M3X4),
+                lhsT_scale=q_scales[:, features],
                 rhs=g_codes[c][:, cols].bitcast(E5M2X4),
                 rhs_scale=g_scales[c][:, cols],
                 start=(c == 0),
@@ -81,61 +83,72 @@ def tile_attend_dk_kernel(tc, g, qm, offs, out):
                 raw.rearrange("p j (b i) -> p b j i", i=4),
             )
 
-        def cast_pair(copy, c, raw, h, first, lo, hi):
+        def cast_first(copy, lo, hi):
+            cast_words(copy, gb[0][:, lo:hi, :], g0[:, :, lo:hi])
+
+        def cast_q(copy, c):
+            cast_words(copy, qb[:, c * D : (c + 1) * D, :], q_raw[:, c, :].rearrange("p (j d) -> p j d", j=PACK))
+
+        def cast_pair(copy, h, lo, hi):
             copy(
-                gb[c][:, lo:hi, 2 * h : 2 * h + 2],
-                raw[:, :, lo - first : hi - first].rearrange("p j w -> p w j"),
+                gb[1][:, lo:hi, 2 * h : 2 * h + 2],
+                g1[:, 2 * h : 2 * h + 2, lo:hi].rearrange("p j w -> p w j"),
             )
 
-        def copy_out(copy, k):
-            copy(sums[:, k * GROUP : (k + 1) * GROUP], acc[k][:])
+        def cast_late_pairs(groups):
+            for copy, lo, hi in ((v, 0, LATE_ON_VECTOR), (s, LATE_ON_VECTOR, GROUP)):
+                for k in groups:
+                    cast_pair(copy, 1, k * GROUP + lo, k * GROUP + hi)
 
-        half = SLOTS // 2
-        q_raw = load(qm_rows, "q_raw")
-        g0 = load(g_rows[0], "g_raw0")
-        last = held.tile([P, PACK * SLOTS], F32, name="g_raw1", align_bytes=4096)
-        g1 = last[:].rearrange("p (j n) -> p j n", j=PACK)
-        early = SLOTS + half
-        nc.sync.dma_start(out=last[:, :early], in_=g_rows[1].rearrange("p j n -> p (j n)")[:, :early])
-        nc.sync.dma_start(out=g1[:, 2:, :half], in_=g_rows[1][:, 2:, :half])
-        nc.sync.dma_start(out=g1[:, 1:, half:], in_=g_rows[1][:, 1:, half:])
-        sums = last[:, 2 * SLOTS - 16 : 3 * SLOTS - 16]
+        def copy_out(k):
+            s(sums[:, k * GROUP : (k + 1) * GROUP], acc[k][:])
+
+        nc.sync.dma_start(out=g0[:], in_=g_rows[0])
+        nc.sync.dma_start(out=q_raw[:], in_=qm_rows)
+        early = SLOTS + HALF
+        nc.sync.dma_start(out=last[:, :early], in_=g1_run[:, :early])
+        nc.sync.dma_start(out=g1[:, 2:, :HALF], in_=g_rows[1][:, 2:, :HALF])
+        nc.sync.dma_start(out=last[:, early : 2 * SLOTS], in_=g1_run[:, early : 2 * SLOTS])
+        nc.sync.dma_start(out=g1[:, 2:, HALF:], in_=g_rows[1][:, 2:, HALF:])
         nc.sync.dma_start(offsets[:], offs)
+        sums = last[:, 2 * SLOTS + HALF : 3 * SLOTS + HALF]
 
-        nc.vector.memset(low[:, HEAD:], 0.0)
+        nc.vector.memset(main[:, HEAD:], 0.0)
         nc.vector.memset(head[:, :HEAD], 0.0)
 
-        for c, copy in ((0, s), (1, v)):
-            cast_words(copy, qb[c][:], q_raw[:, c, :].rearrange("p (j d) -> p j d", j=PACK))
-        quantize_q(1)
-        quantize_q(0)
-        for copy, lo, hi in ((v, 0, GROUP), (v, GROUP, half), (v, half, 304), (s, 304, 384), (s, 384, SLOTS)):
-            cast_words(copy, gb[0][:, lo:hi, :], g0[:, :, lo:hi])
-        for k in range(GROUPS):
-            quantize_g(0, k * GROUP, (k + 1) * GROUP)
+        for k, copy in enumerate((v, v, s, s)):
+            cast_first(copy, k * GROUP, (k + 1) * GROUP)
+        quantize_g(0, 0)
+        quantize_g(0, 1)
+        for c in range(PASSES):
+            cast_q(v, c)
+        quantize_g(0, 2)
+        quantize(qb, q_codes, q_scales, 0, PASSES * D, E4M3X4)
+        for k in range(3):
             multiply(0, k)
 
-        cast_pair(s, 1, g1[:, :2, :], 0, 0, 0, GROUP)
-        cast_pair(v, 1, g1[:, 2:, :], 1, 0, 0, 96)
-        cast_pair(s, 1, g1[:, 2:, :], 1, 0, 96, GROUP)
-        for copy, lo, hi in ((v, GROUP, 216), (s, 216, half)):
-            cast_words(copy, gb[1][:, lo:hi, :], g1[:, :, lo:hi])
+        cast_pair(v, 0, 0, LOW_EARLY_ON_VECTOR)
+        cast_pair(s, 0, LOW_EARLY_ON_VECTOR, HALF)
+        cast_late_pairs((0, 1))
+        cast_pair(s, 0, SLOTS - HIGH_EARLY_ON_SCALAR, SLOTS)
+        quantize_g(0, 3)
+        multiply(0, 3)
         for k in (0, 1):
-            quantize_g(1, k * GROUP, (k + 1) * GROUP)
+            quantize_g(1, k)
             multiply(1, k)
-        for copy, lo, hi in ((v, half, 352), (v, 384, 464), (s, 496, SLOTS), (s, 352, 384), (s, 464, 496)):
-            cast_words(copy, gb[1][:, lo:hi, :], g1[:, :, lo:hi])
+        cast_pair(v, 0, HALF, SLOTS - HIGH_EARLY_ON_SCALAR)
+        cast_late_pairs((2, 3))
         for k in (2, 3):
-            quantize_g(1, k * GROUP, (k + 1) * GROUP)
+            quantize_g(1, k)
             multiply(1, k)
 
-        copy_out(s, 0)
-        copy_out(s, 1)
+        copy_out(0)
+        copy_out(1)
         nc.scalar.activation(head[:].indirect(offsets[:, : GROUP // 16]), sums[:, :GROUP], COPY)
-        copy_out(s, 2)
-        copy_out(s, 3)
+        copy_out(2)
+        copy_out(3)
         nc.scalar.activation(head[:].indirect(offsets[:, GROUP // 16 : HEAD // 16]), sums[:, GROUP:HEAD], COPY)
-        for lo in (0, half):
-            nc.vector.tensor_copy(low[:].indirect(offsets[:, lo // 16 : (lo + half) // 16]), sums[:, lo : lo + half])
-        for window, cols in ((head, slice(0, HEAD)), (low, slice(HEAD, TOKENS))):
+        for lo in (0, HALF):
+            nc.vector.tensor_copy(main[:].indirect(offsets[:, lo // 16 : (lo + HALF) // 16]), sums[:, lo : lo + HALF])
+        for window, cols in ((head, slice(0, HEAD)), (main, slice(HEAD, TOKENS))):
             nc.sync.dma_start(out=out[:, cols], in_=window[:, cols])

@@ -22,9 +22,11 @@ GROUP = 128
 GROUPS = SLOTS // GROUP
 HALF = SLOTS // 2
 HEAD = 320
-LOW_EARLY_ON_VECTOR = 64
-LATE_ON_VECTOR = 88
-HIGH_EARLY_ON_SCALAR = 192
+FIRST_ON_VECTOR = 352
+LOW_ON_VECTOR = 88
+PITCH = 448
+EDGE = HALF - (PITCH - HALF) // 2 - GROUP
+THIRD_ON_SCALAR = 40
 
 
 def tile_attend_dk_kernel(tc, g, qm, offs, out):
@@ -43,15 +45,15 @@ def tile_attend_dk_kernel(tc, g, qm, offs, out):
 
         g_codes = [held.tile([P, SLOTS], U32, name=f"g_codes{c}", align_bytes=256) for c in range(PASSES)]
         g_scales = [held.tile([P, SLOTS], U8, name=f"g_scales{c}", align_bytes=256) for c in range(PASSES)]
-        q_codes = held.tile([P, PASSES * D], U32, name="q_codes", align_bytes=256)
-        q_scales = held.tile([P, PASSES * D], U8, name="q_scales", align_bytes=256)
+        q_codes = [held.tile([P, D], U32, name=f"q_codes{c}", align_bytes=256) for c in range(PASSES)]
+        q_scales = [held.tile([P, D], U8, name=f"q_scales{c}", align_bytes=256) for c in range(PASSES)]
         gb = [held.tile([P, SLOTS, PACK], BF16, name=f"gb{c}", align_bytes=256) for c in range(PASSES)]
-        qb = held.tile([P, PASSES * D, PACK], BF16, name="qb", align_bytes=256)
-        g0 = held.tile([P, PACK, SLOTS], F32, name="g_raw0", align_bytes=4096)
+        qb = [held.tile([P, D, PACK], BF16, name=f"qb{c}", align_bytes=256) for c in range(PASSES)]
+        g0 = [held.tile([P, 2, SLOTS], F32, name=f"g_raw0{h}", align_bytes=4096) for h in range(2)]
         q_raw = held.tile([P, PASSES, PACK * D], F32, name="q_raw", align_bytes=4096)
-        last = held.tile([P, PACK * SLOTS], F32, name="g_raw1", align_bytes=4096)
-        g1 = last[:].rearrange("p (j n) -> p j n", j=PACK)
-        g1_run = g_rows[1].rearrange("p j n -> p (j n)")
+        low = held.tile([P, PACK, HALF], F32, name="g_low", align_bytes=4096)
+        spaced = held.tile([P, PACK * PITCH], F32, name="g_high", align_bytes=4096)
+        high = spaced[:].rearrange("p (j n) -> p j n", j=PACK)[:, :, :HALF]
         v, s = nc.vector.tensor_copy, nc.scalar.copy
 
         def quantize(grouped, codes, scales, lo, hi, dtype):
@@ -64,13 +66,15 @@ def tile_attend_dk_kernel(tc, g, qm, offs, out):
         def quantize_g(c, k):
             quantize(gb[c], g_codes[c], g_scales[c], k * GROUP, (k + 1) * GROUP, E5M2X4)
 
+        def quantize_q(c):
+            quantize(qb[c], q_codes[c], q_scales[c], 0, D, E4M3X4)
+
         def multiply(c, k):
             cols = slice(k * GROUP, (k + 1) * GROUP)
-            features = slice(c * D, (c + 1) * D)
             nc.tensor.matmul_mx(
                 out=acc[k][:],
-                lhsT=q_codes[:, features].bitcast(E4M3X4),
-                lhsT_scale=q_scales[:, features],
+                lhsT=q_codes[c][:].bitcast(E4M3X4),
+                lhsT_scale=q_scales[c][:],
                 rhs=g_codes[c][:, cols].bitcast(E5M2X4),
                 rhs_scale=g_scales[c][:, cols],
                 start=(c == 0),
@@ -83,61 +87,54 @@ def tile_attend_dk_kernel(tc, g, qm, offs, out):
                 raw.rearrange("p j (b i) -> p b j i", i=4),
             )
 
-        def cast_first(copy, lo, hi):
-            cast_words(copy, gb[0][:, lo:hi, :], g0[:, :, lo:hi])
+        def cast_first(copy, h, lo, hi):
+            copy(gb[0][:, lo:hi, 2 * h : 2 * h + 2], g0[h][:, :, lo:hi].rearrange("p j w -> p w j"))
 
         def cast_q(copy, c):
-            cast_words(copy, qb[:, c * D : (c + 1) * D, :], q_raw[:, c, :].rearrange("p (j d) -> p j d", j=PACK))
+            cast_words(copy, qb[c][:], q_raw[:, c, :].rearrange("p (j d) -> p j d", j=PACK))
 
-        def cast_pair(copy, h, lo, hi):
-            copy(
-                gb[1][:, lo:hi, 2 * h : 2 * h + 2],
-                g1[:, 2 * h : 2 * h + 2, lo:hi].rearrange("p j w -> p w j"),
-            )
-
-        def cast_late_pairs(groups):
-            for copy, lo, hi in ((v, 0, LATE_ON_VECTOR), (s, LATE_ON_VECTOR, GROUP)):
-                for k in groups:
-                    cast_pair(copy, 1, k * GROUP + lo, k * GROUP + hi)
+        def cast_last(copy, raw, first, lo, hi):
+            cast_words(copy, gb[1][:, first + lo : first + hi, :], raw[:, :, lo:hi])
 
         def copy_out(k):
             s(sums[:, k * GROUP : (k + 1) * GROUP], acc[k][:])
 
-        nc.sync.dma_start(out=g0[:], in_=g_rows[0])
+        for h in range(2):
+            nc.sync.dma_start(out=g0[h][:], in_=g_rows[0][:, 2 * h : 2 * h + 2, :])
         nc.sync.dma_start(out=q_raw[:], in_=qm_rows)
-        early = SLOTS + HALF
-        nc.sync.dma_start(out=last[:, :early], in_=g1_run[:, :early])
-        nc.sync.dma_start(out=g1[:, 2:, :HALF], in_=g_rows[1][:, 2:, :HALF])
-        nc.sync.dma_start(out=last[:, early : 2 * SLOTS], in_=g1_run[:, early : 2 * SLOTS])
-        nc.sync.dma_start(out=g1[:, 2:, HALF:], in_=g_rows[1][:, 2:, HALF:])
+        nc.sync.dma_start(out=low[:], in_=g_rows[1][:, :, :HALF])
+        nc.sync.dma_start(out=high, in_=g_rows[1][:, :, HALF:])
         nc.sync.dma_start(offsets[:], offs)
-        sums = last[:, 2 * SLOTS + HALF : 3 * SLOTS + HALF]
+        sums = spaced[:, HALF - EDGE : HALF - EDGE + SLOTS]
 
         nc.vector.memset(main[:, HEAD:], 0.0)
         nc.vector.memset(head[:, :HEAD], 0.0)
 
-        for k, copy in enumerate((v, v, s, s)):
-            cast_first(copy, k * GROUP, (k + 1) * GROUP)
-        quantize_g(0, 0)
-        quantize_g(0, 1)
-        for c in range(PASSES):
-            cast_q(v, c)
-        quantize_g(0, 2)
-        quantize(qb, q_codes, q_scales, 0, PASSES * D, E4M3X4)
+        cast_first(v, 0, 0, FIRST_ON_VECTOR)
+        cast_first(s, 0, FIRST_ON_VECTOR, SLOTS)
+        cast_first(v, 1, 0, GROUP)
+        cast_first(v, 1, GROUP, FIRST_ON_VECTOR)
+        cast_first(s, 1, FIRST_ON_VECTOR, SLOTS)
         for k in range(3):
+            quantize_g(0, k)
+        cast_q(v, 0)
+        cast_q(s, 1)
+        quantize_g(0, 3)
+        for c in range(PASSES):
+            quantize_q(c)
+        for k in range(GROUPS):
             multiply(0, k)
 
-        cast_pair(v, 0, 0, LOW_EARLY_ON_VECTOR)
-        cast_pair(s, 0, LOW_EARLY_ON_VECTOR, HALF)
-        cast_late_pairs((0, 1))
-        cast_pair(s, 0, SLOTS - HIGH_EARLY_ON_SCALAR, SLOTS)
-        quantize_g(0, 3)
-        multiply(0, 3)
+        for copy, lo, hi in ((v, 0, LOW_ON_VECTOR), (s, LOW_ON_VECTOR, GROUP)):
+            for k in (0, 1):
+                cast_last(copy, low, 0, k * GROUP + lo, k * GROUP + hi)
         for k in (0, 1):
             quantize_g(1, k)
             multiply(1, k)
-        cast_pair(v, 0, HALF, SLOTS - HIGH_EARLY_ON_SCALAR)
-        cast_late_pairs((2, 3))
+        cast_last(s, high, HALF, HALF - EDGE, HALF)
+        cast_last(s, high, HALF, 0, THIRD_ON_SCALAR)
+        cast_last(v, high, HALF, THIRD_ON_SCALAR, GROUP)
+        cast_last(v, high, HALF, GROUP, HALF - EDGE)
         for k in (2, 3):
             quantize_g(1, k)
             multiply(1, k)

@@ -21,12 +21,10 @@ PASSES = Q // (P * PACK)
 GROUP = 128
 GROUPS = SLOTS // GROUP
 HALF = SLOTS // 2
-HEAD = 320
-FIRST_ON_VECTOR = 352
+HEAD = 384
 LOW_ON_VECTOR = 88
-PITCH = 448
-EDGE = HALF - (PITCH - HALF) // 2 - GROUP
-THIRD_ON_SCALAR = 40
+LAST_ON_VECTOR = 80
+EDGE = 32
 
 
 def tile_attend_dk_kernel(tc, g, qm, offs, out):
@@ -49,11 +47,12 @@ def tile_attend_dk_kernel(tc, g, qm, offs, out):
         q_scales = [held.tile([P, D], U8, name=f"q_scales{c}", align_bytes=256) for c in range(PASSES)]
         gb = [held.tile([P, SLOTS, PACK], BF16, name=f"gb{c}", align_bytes=256) for c in range(PASSES)]
         qb = [held.tile([P, D, PACK], BF16, name=f"qb{c}", align_bytes=256) for c in range(PASSES)]
-        g0 = [held.tile([P, 2, SLOTS], F32, name=f"g_raw0{h}", align_bytes=4096) for h in range(2)]
         q_raw = held.tile([P, PASSES, PACK * D], F32, name="q_raw", align_bytes=4096)
         low = held.tile([P, PACK, HALF], F32, name="g_low", align_bytes=4096)
-        spaced = held.tile([P, PACK * PITCH], F32, name="g_high", align_bytes=4096)
-        high = spaced[:].rearrange("p (j n) -> p j n", j=PACK)[:, :, :HALF]
+        opening = held.tile([P, PACK, HALF], F32, name="opening", align_bytes=4096)
+        shared = held.tile([P, PASSES * PACK * HALF], F32, name="shared", align_bytes=4096)
+        g0 = [opening[:], shared[:, : PACK * HALF].rearrange("p (j n) -> p j n", j=PACK)]
+        high = shared[:, PACK * HALF :].rearrange("p (j n) -> p j n", j=PACK)
         v, s = nc.vector.tensor_copy, nc.scalar.copy
 
         def quantize(grouped, codes, scales, lo, hi, dtype):
@@ -88,7 +87,7 @@ def tile_attend_dk_kernel(tc, g, qm, offs, out):
             )
 
         def cast_first(copy, h, lo, hi):
-            copy(gb[0][:, lo:hi, 2 * h : 2 * h + 2], g0[h][:, :, lo:hi].rearrange("p j w -> p w j"))
+            cast_words(copy, gb[0][:, h * HALF + lo : h * HALF + hi, :], g0[h][:, :, lo:hi])
 
         def cast_q(copy, c):
             cast_words(copy, qb[c][:], q_raw[:, c, :].rearrange("p (j d) -> p j d", j=PACK))
@@ -99,30 +98,28 @@ def tile_attend_dk_kernel(tc, g, qm, offs, out):
         def copy_out(k):
             s(sums[:, k * GROUP : (k + 1) * GROUP], acc[k][:])
 
-        for h in range(2):
-            nc.sync.dma_start(out=g0[h][:], in_=g_rows[0][:, 2 * h : 2 * h + 2, :])
+        nc.sync.dma_start(out=g0[0], in_=g_rows[0][:, :, :HALF])
         nc.sync.dma_start(out=q_raw[:], in_=qm_rows)
         nc.sync.dma_start(out=low[:], in_=g_rows[1][:, :, :HALF])
+        nc.sync.dma_start(out=g0[1], in_=g_rows[0][:, :, HALF:])
         nc.sync.dma_start(out=high, in_=g_rows[1][:, :, HALF:])
         nc.sync.dma_start(offsets[:], offs)
-        sums = spaced[:, HALF - EDGE : HALF - EDGE + SLOTS]
+        first = PACK * HALF - HALF + EDGE
+        sums = shared[:, first : first + SLOTS]
 
         nc.vector.memset(main[:, HEAD:], 0.0)
         nc.vector.memset(head[:, :HEAD], 0.0)
 
-        cast_first(v, 0, 0, FIRST_ON_VECTOR)
-        cast_first(s, 0, FIRST_ON_VECTOR, SLOTS)
-        cast_first(v, 1, 0, GROUP)
-        cast_first(v, 1, GROUP, FIRST_ON_VECTOR)
-        cast_first(s, 1, FIRST_ON_VECTOR, SLOTS)
-        for k in range(3):
+        cast_first(v, 0, 0, GROUP)
+        cast_first(v, 0, GROUP, GROUP + LOW_ON_VECTOR)
+        cast_first(s, 0, GROUP + LOW_ON_VECTOR, HALF)
+        for k in (0, 1):
             quantize_g(0, k)
         cast_q(v, 0)
         cast_q(s, 1)
-        quantize_g(0, 3)
         for c in range(PASSES):
             quantize_q(c)
-        for k in range(GROUPS):
+        for k in (0, 1):
             multiply(0, k)
 
         for copy, lo, hi in ((v, 0, LOW_ON_VECTOR), (s, LOW_ON_VECTOR, GROUP)):
@@ -131,20 +128,27 @@ def tile_attend_dk_kernel(tc, g, qm, offs, out):
         for k in (0, 1):
             quantize_g(1, k)
             multiply(1, k)
-        cast_last(s, high, HALF, HALF - EDGE, HALF)
-        cast_last(s, high, HALF, 0, THIRD_ON_SCALAR)
-        cast_last(v, high, HALF, THIRD_ON_SCALAR, GROUP)
-        cast_last(v, high, HALF, GROUP, HALF - EDGE)
+        for copy, lo, hi in ((v, 0, LOW_ON_VECTOR), (s, LOW_ON_VECTOR, GROUP)):
+            for k in (0, 1):
+                cast_first(copy, 1, k * GROUP + lo, k * GROUP + hi)
+        copy_out(0)
+        s(sums[:, GROUP : HALF - EDGE], acc[1][:, : GROUP - EDGE])
+        for k in (2, 3):
+            quantize_g(0, k)
+            multiply(0, k)
+        for copy, lo, hi in ((v, 0, LAST_ON_VECTOR), (s, LAST_ON_VECTOR, GROUP)):
+            for k in (0, 1):
+                cast_last(copy, high, HALF, k * GROUP + lo, k * GROUP + hi)
+        v(sums[:, HALF - EDGE : HALF], acc[1][:, GROUP - EDGE :])
         for k in (2, 3):
             quantize_g(1, k)
             multiply(1, k)
 
-        copy_out(0)
-        copy_out(1)
-        nc.scalar.activation(head[:].indirect(offsets[:, : GROUP // 16]), sums[:, :GROUP], COPY)
+        early = HALF - EDGE
+        nc.scalar.activation(head[:].indirect(offsets[:, : early // 16]), sums[:, :early], COPY)
         copy_out(2)
         copy_out(3)
-        nc.scalar.activation(head[:].indirect(offsets[:, GROUP // 16 : HEAD // 16]), sums[:, GROUP:HEAD], COPY)
+        nc.scalar.activation(head[:].indirect(offsets[:, early // 16 : HEAD // 16]), sums[:, early:HEAD], COPY)
         for lo in (0, HALF):
             nc.vector.tensor_copy(main[:].indirect(offsets[:, lo // 16 : (lo + HALF) // 16]), sums[:, lo : lo + HALF])
         for window, cols in ((head, slice(0, HEAD)), (main, slice(HEAD, TOKENS))):

@@ -21,7 +21,7 @@ PASSES = Q // (P * PACK)
 GROUP = 128
 GROUPS = SLOTS // GROUP
 HALF = SLOTS // 2
-HEAD = 384
+HEAD = 352
 LOW_ON_VECTOR = 88
 LAST_ON_VECTOR = 80
 EDGE = 32

@@ -23,7 +23,7 @@ GROUPS = SLOTS // GROUP
 HALF = SLOTS // 2
 HEAD = 352
 LOW_ON_VECTOR = 88
-LAST_ON_VECTOR = 80
+LAST_ON_SCALAR = 64
 EDGE = 32
 
 
@@ -136,10 +136,11 @@ def tile_attend_dk_kernel(tc, g, qm, offs, out):
         for k in (2, 3):
             quantize_g(0, k)
             multiply(0, k)
-        for copy, lo, hi in ((v, 0, LAST_ON_VECTOR), (s, LAST_ON_VECTOR, GROUP)):
-            for k in (0, 1):
-                cast_last(copy, high, HALF, k * GROUP + lo, k * GROUP + hi)
-        v(sums[:, HALF - EDGE : HALF], acc[1][:, GROUP - EDGE :])
+        cast_last(s, high, HALF, 0, EDGE)
+        cast_last(s, high, HALF, HALF - LAST_ON_SCALAR, HALF)
+        cast_last(v, high, HALF, EDGE, GROUP)
+        cast_last(v, high, HALF, GROUP, HALF - LAST_ON_SCALAR)
+        s(sums[:, HALF - EDGE : HALF], acc[1][:, GROUP - EDGE :])
         for k in (2, 3):
             quantize_g(1, k)
             multiply(1, k)

from contextlib import ExitStack

import concourse.mybir as mybir

Q, SLOTS, TOKENS, D = 1024, 512, 1024, 128

FLOPS = 2 * Q * SLOTS * D

F32 = mybir.dt.float32
BF16 = mybir.dt.bfloat16
U32 = mybir.dt.uint32
U16 = mybir.dt.uint16
U8 = mybir.dt.uint8
E4M3X4 = mybir.dt.float8_e4m3fn_x4
E5M2X4 = mybir.dt.float8_e5m2_x4
COPY = mybir.ActivationFunctionType.Copy

P = 128
PACK = 4
PASSES = Q // (P * PACK)
GROUP = 128
GROUPS = SLOTS // GROUP
HALF = SLOTS // 2
HEAD = 352
LOW_ON_VECTOR = 88
LAST_ON_SCALAR = 64
EDGE = 32


def tile_attend_dk_kernel(tc, g, qm, offs, out):
    nc = tc.nc
    g_rows = g.rearrange("b (c p j) n -> (b c) p j n", p=P, j=PACK)
    qm_rows = qm.rearrange("b (c p j) d -> p (b c) (j d)", p=P, j=PACK)

    with ExitStack() as ctx:
        held = ctx.enter_context(tc.tile_pool(name="held", bufs=1))
        psum = ctx.enter_context(tc.psum_pool(name="psum", bufs=1))

        offsets = held.tile([P, SLOTS // 16], U16, name="offsets")
        main = held.tile([P, TOKENS], F32, name="main", align_bytes=4096)
        head = held.tile([P, TOKENS], F32, name="head", align_bytes=4096)
        acc = [psum.tile([D, GROUP], F32, name=f"acc{k}") for k in range(GROUPS)]

        g_codes = [held.tile([P, SLOTS], U32, name=f"g_codes{c}", align_bytes=256) for c in range(PASSES)]
        g_scales = [held.tile([P, SLOTS], U8, name=f"g_scales{c}", align_bytes=256) for c in range(PASSES)]
        q_codes = [held.tile([P, D], U32, name=f"q_codes{c}", align_bytes=256) for c in range(PASSES)]
        q_scales = [held.tile([P, D], U8, name=f"q_scales{c}", align_bytes=256) for c in range(PASSES)]
        gb = [held.tile([P, SLOTS, PACK], BF16, name=f"gb{c}", align_bytes=256) for c in range(PASSES)]
        qb = [held.tile([P, D, PACK], BF16, name=f"qb{c}", align_bytes=256) for c in range(PASSES)]
        q_raw = held.tile([P, PASSES, PACK * D], F32, name="q_raw", align_bytes=4096)
        low = held.tile([P, PACK, HALF], F32, name="g_low", align_bytes=4096)
        opening = held.tile([P, PACK, HALF], F32, name="opening", align_bytes=4096)
        shared = held.tile([P, PASSES * PACK * HALF], F32, name="shared", align_bytes=4096)
        g0 = [opening[:], shared[:, : PACK * HALF].rearrange("p (j n) -> p j n", j=PACK)]
        high = shared[:, PACK * HALF :].rearrange("p (j n) -> p j n", j=PACK)
        v, s = nc.vector.tensor_copy, nc.scalar.copy

        def quantize(grouped, codes, scales, lo, hi, dtype):
            nc.vector.quantize_mx(
                out=codes[:, lo:hi].bitcast(dtype),
                scales=scales[:, lo:hi],
                in_=grouped[:, lo:hi, :].rearrange("p w j -> p (w j)"),
            )

        def quantize_g(c, k):
            quantize(gb[c], g_codes[c], g_scales[c], k * GROUP, (k + 1) * GROUP, E5M2X4)

        def quantize_q(c):
            quantize(qb[c], q_codes[c], q_scales[c], 0, D, E4M3X4)

        def multiply(c, k):
            cols = slice(k * GROUP, (k + 1) * GROUP)
            nc.tensor.matmul_mx(
                out=acc[k][:],
                lhsT=q_codes[c][:].bitcast(E4M3X4),
                lhsT_scale=q_scales[c][:],
                rhs=g_codes[c][:, cols].bitcast(E5M2X4),
                rhs_scale=g_scales[c][:, cols],
                start=(c == 0),
                stop=(c == PASSES - 1),
            )

        def cast_words(copy, grouped, raw):
            copy(
                grouped.rearrange("p (b i) j -> p b j i", i=4),
                raw.rearrange("p j (b i) -> p b j i", i=4),
            )

        def cast_first(copy, h, lo, hi):
            cast_words(copy, gb[0][:, h * HALF + lo : h * HALF + hi, :], g0[h][:, :, lo:hi])

        def cast_q(copy, c):
            cast_words(copy, qb[c][:], q_raw[:, c, :].rearrange("p (j d) -> p j d", j=PACK))

        def cast_last(copy, raw, first, lo, hi):
            cast_words(copy, gb[1][:, first + lo : first + hi, :], raw[:, :, lo:hi])

        def copy_out(k):
            s(sums[:, k * GROUP : (k + 1) * GROUP], acc[k][:])

        nc.sync.dma_start(out=g0[0], in_=g_rows[0][:, :, :HALF])
        nc.sync.dma_start(out=q_raw[:], in_=qm_rows)
        nc.sync.dma_start(out=low[:], in_=g_rows[1][:, :, :HALF])
        nc.sync.dma_start(out=g0[1], in_=g_rows[0][:, :, HALF:])
        nc.sync.dma_start(out=high, in_=g_rows[1][:, :, HALF:])
        nc.sync.dma_start(offsets[:], offs)
        first = PACK * HALF - HALF + EDGE
        sums = shared[:, first : first + SLOTS]

        nc.vector.memset(main[:, HEAD:], 0.0)
        nc.vector.memset(head[:, :HEAD], 0.0)

        cast_first(v, 0, 0, GROUP)
        cast_first(v, 0, GROUP, GROUP + LOW_ON_VECTOR)
        cast_first(s, 0, GROUP + LOW_ON_VECTOR, HALF)
        for k in (0, 1):
            quantize_g(0, k)
        cast_q(v, 0)
        cast_q(s, 1)
        for c in range(PASSES):
            quantize_q(c)
        for k in (0, 1):
            multiply(0, k)

        for copy, lo, hi in ((v, 0, LOW_ON_VECTOR), (s, LOW_ON_VECTOR, GROUP)):
            for k in (0, 1):
                cast_last(copy, low, 0, k * GROUP + lo, k * GROUP + hi)
        for k in (0, 1):
            quantize_g(1, k)
            multiply(1, k)
        for copy, lo, hi in ((v, 0, LOW_ON_VECTOR), (s, LOW_ON_VECTOR, GROUP)):
            for k in (0, 1):
                cast_first(copy, 1, k * GROUP + lo, k * GROUP + hi)
        copy_out(0)
        s(sums[:, GROUP : HALF - EDGE], acc[1][:, : GROUP - EDGE])
        for k in (2, 3):
            quantize_g(0, k)
            multiply(0, k)
        cast_last(s, high, HALF, 0, EDGE)
        cast_last(s, high, HALF, HALF - LAST_ON_SCALAR, HALF)
        cast_last(v, high, HALF, EDGE, GROUP)
        cast_last(v, high, HALF, GROUP, HALF - LAST_ON_SCALAR)
        s(sums[:, HALF - EDGE : HALF], acc[1][:, GROUP - EDGE :])
        for k in (2, 3):
            quantize_g(1, k)
            multiply(1, k)

        early = HALF - EDGE
        nc.scalar.activation(head[:].indirect(offsets[:, : early // 16]), sums[:, :early], COPY)
        copy_out(2)
        copy_out(3)
        nc.scalar.activation(head[:].indirect(offsets[:, early // 16 : HEAD // 16]), sums[:, early:HEAD], COPY)
        for lo in (0, HALF):
            nc.vector.tensor_copy(main[:].indirect(offsets[:, lo // 16 : (lo + HALF) // 16]), sums[:, lo : lo + HALF])
        for window, cols in ((head, slice(0, HEAD)), (main, slice(HEAD, TOKENS))):
            nc.sync.dma_start(out=out[:, cols], in_=window[:, cols])
